import numpy as np
import ml_dtypes


def mxq(x, axis, fmt="e4m3"):
    dtype, down = {"e4m3": (ml_dtypes.float8_e4m3fn, 7), "e5m2": (ml_dtypes.float8_e5m2, 14)}[fmt]
    v = np.moveaxis(np.asarray(x, np.float32).astype(ml_dtypes.bfloat16).astype(np.float64), axis, -1)
    blocks = v.reshape(v.shape[:-1] + (-1, 32))
    amax = np.abs(blocks).max(-1, keepdims=True)
    byte = np.maximum(np.where(amax > 0, np.frexp(amax)[1] - 1 + 127, 0) - down, 1)
    scale = np.exp2(byte - 127.0)
    codes = (blocks / scale).astype(np.float32).astype(dtype).astype(np.float64)
    return np.moveaxis((codes * scale).reshape(v.shape), -1, axis)


WIDE = False


def mx_kscale(k):
    if not WIDE:
        return np.ones(k)
    levels = np.array([10, -10, 5, -5, 0])
    if k % 512:
        return np.exp2(np.random.permutation(np.resize(levels, k // 32))).repeat(32)
    a = np.empty((k // 512, 16))
    for p in range(k // 512):
        a[p, :8] = np.random.permutation(np.resize(levels, 8))
        for g in range(8):
            far = levels[np.abs(levels - a[p, g]) >= 10]
            a[p, g + 8] = far[np.random.randint(len(far))]
    return np.exp2(a.ravel()).repeat(32)


def f64(x):
    return np.asarray(x).astype(np.float64)


def striped(idx):
    return np.tile(idx.reshape(-1, 16).T, (8, 1)).astype(np.uint16)


def unstriped(offs):
    return offs[:16].T.reshape(-1).astype(np.int64)


E2M1 = np.array([0.0, 0.5, 1.0, 1.5, 2.0, 3.0, 4.0, 6.0, -0.0, -0.5, -1.0, -1.5, -2.0, -3.0, -4.0, -6.0])


def pack_fp4(w):
    k, n = w.shape
    w = f64(np.asarray(w, np.float32).astype(ml_dtypes.bfloat16)).reshape(k // 32, 32, n)
    amax = np.abs(w).max(1)
    mant, ex = np.frexp(amax / 6.0)
    byte = np.clip(np.where(amax > 0, np.where(mant > 0.5, ex, ex - 1) + 127, 1), 1, 254)
    scaled = (w * np.exp2(127.0 - byte)[:, None, :]).reshape(k, n).astype(np.float32)
    c = np.ascontiguousarray(scaled.reshape(k // 512, 128, 4, n).transpose(0, 1, 3, 2)).astype(ml_dtypes.float4_e2m1fn).view(np.uint8) & 0xF
    words = (c[..., 0::2] | (c[..., 1::2] << 4)).reshape(k // 512, 128, 2 * n)
    return np.ascontiguousarray(words), np.ascontiguousarray(byte.astype(np.uint8).reshape(k // 512, 16, n))


def unpack_fp4(words, scales):
    g, _, n = scales.shape
    words = np.ascontiguousarray(words).reshape(g, 128, n, 2)
    nib = np.empty((g, 128, n, 4), np.uint8)
    nib[..., 0::2] = words & 0xF
    nib[..., 1::2] = words >> 4
    vals = E2M1[nib] * np.repeat(np.exp2(scales.astype(np.float64) - 127.0), 8, axis=1)[..., None]
    return vals.transpose(0, 1, 3, 2).reshape(g * 512, n)


def silu(v):
    return v / (1.0 + np.exp(-np.maximum(v, -700.0)))


K, T, S, D, H, N = 1024, 1024, 512, 4, 512, 256


def setup_inputs():
    n = np.random.standard_normal
    s = mx_kscale(K)[:, None]
    u = mx_kscale(H)
    packed_xT = pack_fp4(n((K, T)) * s)
    return {
        "x_words": packed_xT[0],
        "x_scales": packed_xT[1],
        "w1": (n((K, H)) / np.sqrt(K) / s * u).astype(np.float32),
        "w2": (n((H, N)) / np.sqrt(H) / u[:, None]).astype(np.float32),
        "taps": (n((H, D)) / np.sqrt(D)).astype(np.float32),
        "offs": striped(np.random.permutation(T)[:S]),
    }


def reference(x_words, x_scales, w1, w2, taps, offs):
    xq = unpack_fp4(x_words, x_scales)[:, unstriped(offs)]
    h = mxq(f64(w1), 0, "e4m3").T @ xq
    z = silu(f64(taps)[:, 0:1] * h + f64(taps)[:, 1:2] * (np.pad(h, ((0, 0), (1, 0)))[:, :S]) + f64(taps)[:, 2:3] * (np.pad(h, ((0, 0), (2, 0)))[:, :S]) + f64(taps)[:, 3:4] * (np.pad(h, ((0, 0), (3, 0)))[:, :S]))
    return mxq(f64(w2), 0, "e4m3").T @ mxq(z, 0, "e4m3")

@@ -1,0 +1,179 @@
+from contextlib import ExitStack
+
+import concourse.mybir as mybir
+
+K, T, S, D, H, N = 1024, 1024, 512, 4, 512, 256
+FLOPS = 2 * K * H * S + 2 * H * N * S
+
+F32 = mybir.dt.float32
+BF16 = mybir.dt.bfloat16
+I32 = mybir.dt.int32
+U32 = mybir.dt.uint32
+U16 = mybir.dt.uint16
+U8 = mybir.dt.uint8
+FP8X4 = mybir.dt.float8_e4m3fn_x4
+FP4X4 = mybir.dt.float4_e2m1fn_x4
+MULT = mybir.AluOpType.mult
+ADD = mybir.AluOpType.add
+COPY = mybir.ActivationFunctionType.Copy
+SILU = mybir.ActivationFunctionType.Silu
+
+P = 128
+PACK = 4
+K_PASS = P * PACK
+PASSES = K // K_PASS
+QUADRANT = 32
+CHUNKS = ((0, 256), (256, 384), (384, 512))
+M_VECTOR = 84
+
+
+def tile_picked_dconv_silu_p_kernel(tc, x_words, x_scales, w1, w2, taps, offs, out):
+    nc = tc.nc
+    with ExitStack() as ctx:
+        keep = ctx.enter_context(tc.tile_pool(name="keep", bufs=1))
+        psum = ctx.enter_context(tc.psum_pool(name="psum", bufs=1))
+
+        offsets = keep.tile([P, S // 16], U16, name="offsets")
+        words = [keep.tile([P, T], U16, name=f"words{g}", align_bytes=64) for g in range(PASSES)]
+        scales = keep.tile([P, PASSES, T], U8, name="scales", align_bytes=64)
+        w1_raw = [keep.tile([P, PACK, H], F32, name=f"w1_raw{g}", align_bytes=64) for g in range(PASSES)]
+        w2_raw = keep.tile([P, PACK, N], F32, name="w2_raw", align_bytes=64)
+        tap = keep.tile([P, PACK * D], F32, name="tap")
+        zero_in = keep.tile([P, 1], F32, name="zero_in")
+        zero_bias = keep.tile([P, 1], F32, name="zero_bias")
+
+        nc.vector.memset(scales[:].rearrange("p g c -> p (g c)").bitcast(I32), 0)
+        nc.vector.memset(zero_in[:], 0.0)
+        nc.scalar.activation(zero_bias[:], zero_in[:], SILU)
+
+        nc.sync.dma_start(offsets[:], offs)
+        nc.sync.dma_start(words[0][:].bitcast(I32), x_words[0].bitcast(I32))
+        nc.sync.dma_start(tap[:], taps.rearrange("(p t) d -> p (t d)", t=PACK))
+        for q in range(P // QUADRANT):
+            nc.sync.dma_start(
+                scales[QUADRANT * q : QUADRANT * q + 4, :, :].bitcast(I32),
+                x_scales[:, 4 * q : 4 * q + 4, :].rearrange("g r c -> r g c").bitcast(I32),
+            )
+        nc.sync.dma_start(w1_raw[0][:], w1[0:K_PASS, :].rearrange("(p j) c -> p j c", j=PACK))
+        nc.sync.dma_start(words[1][:].bitcast(I32), x_words[1].bitcast(I32))
+        nc.sync.dma_start(w1_raw[1][:], w1[K_PASS:K, :].rearrange("(p j) c -> p j c", j=PACK))
+        nc.sync.dma_start(w2_raw[:], w2.rearrange("(p j) c -> p j c", j=PACK))
+
+        picked_words = [keep.tile([P, S], U16, name=f"picked_words{g}", align_bytes=64) for g in range(PASSES)]
+        picked_scales = [keep.tile([P, S], U8, name=f"picked_scales{g}", align_bytes=64) for g in range(PASSES)]
+        w1_bf = [keep.tile([P, PACK, P, PACK], BF16, name=f"w1_bf{g}", align_bytes=64) for g in range(PASSES)]
+        w1_codes = [[keep.tile([P, P], U32, name=f"w1_codes{g}_{t}", align_bytes=64) for t in range(PACK)] for g in range(PASSES)]
+        w1_scales = [[keep.tile([P, P], U8, name=f"w1_scales{g}_{t}", align_bytes=64) for t in range(PACK)] for g in range(PASSES)]
+        h = [psum.tile([P, S], F32, name=f"h{t}") for t in range(PACK)]
+
+        def cast_w1(copy, g, m0, m1, t0, t1):
+            copy(
+                w1_bf[g][:, t0:t1, m0:m1, :].rearrange("p t m j -> p m j t"),
+                w1_raw[g][:].rearrange("p j (m t) -> p m j t", t=PACK)[:, m0:m1, :, t0:t1],
+            )
+
+        def first_product(g, t):
+            nc.vector.quantize_mx(
+                out=w1_codes[g][t][:].bitcast(FP8X4),
+                scales=w1_scales[g][t][:],
+                in_=w1_bf[g][:, t, :, :].rearrange("p m j -> p (m j)"),
+            )
+            nc.tensor.matmul_mx(
+                out=h[t][:],
+                lhsT=w1_codes[g][t][:].bitcast(FP8X4),
+                lhsT_scale=w1_scales[g][t][:],
+                rhs=picked_words[g][:].bitcast(FP4X4),
+                rhs_scale=picked_scales[g][:],
+                start=(g == 0),
+                stop=(g == PASSES - 1),
+            )
+
+        nc.vector.tensor_copy(picked_words[0][:], words[0][:].indirect(offsets[:]))
+        nc.vector.tensor_copy(picked_scales[0][:], scales[:, 0, :].indirect(offsets[:]))
+        for t0 in (0, 2):
+            cast_w1(nc.scalar.copy, 0, 0, P, t0, t0 + 2)
+            first_product(0, t0)
+            first_product(0, t0 + 1)
+        nc.vector.tensor_copy(picked_scales[1][:], scales[:, 1, :].indirect(offsets[:]))
+        nc.vector.tensor_copy(picked_words[1][:], words[1][:].indirect(offsets[:]))
+        cast_w1(nc.vector.tensor_copy, 1, 0, M_VECTOR, 0, PACK)
+        cast_w1(nc.scalar.copy, 1, M_VECTOR, P, 0, PACK)
+        for t in range(PACK):
+            first_product(1, t)
+
+        u = [keep.tile([P, PACK, c1 - c0], F32, name=f"u{c0}", align_bytes=64) for c0, c1 in CHUNKS]
+        z = [keep.tile([P, c1 - c0, PACK], BF16, name=f"z{c0}", align_bytes=64) for c0, c1 in CHUNKS]
+        z_codes = [keep.tile([P, c1 - c0], U32, name=f"z_codes{c0}", align_bytes=64) for c0, c1 in CHUNKS]
+        z_scales = [keep.tile([P, c1 - c0], U8, name=f"z_scales{c0}", align_bytes=64) for c0, c1 in CHUNKS]
+        w2_bf = keep.tile([P, N, PACK], BF16, name="w2_bf", align_bytes=64)
+        w2_codes = keep.tile([P, N], U32, name="w2_codes", align_bytes=64)
+        w2_scales = keep.tile([P, N], U8, name="w2_scales", align_bytes=64)
+        out_rows = out.rearrange("(b p) j -> p b j", p=P)
+
+        def first_tap(c, t):
+            c0, c1 = CHUNKS[c]
+            nc.scalar.activation(u[c][:, t, :], h[t][:, c0:c1], COPY, scale=tap[:, D * t : D * t + 1])
+
+        def later_taps(c, tiles):
+            c0, c1 = CHUNKS[c]
+            for d in range(1, D):
+                first = max(c0, d)
+                for t in tiles:
+                    nc.vector.scalar_tensor_tensor(
+                        out=u[c][:, t, first - c0 :],
+                        in0=h[t][:, first - d : c1 - d],
+                        scalar=tap[:, D * t + d : D * t + d + 1],
+                        in1=u[c][:, t, first - c0 :],
+                        op0=MULT,
+                        op1=ADD,
+                    )
+
+        def second_product(c):
+            c0, c1 = CHUNKS[c]
+            width = c1 - c0
+            nc.scalar.activation(
+                z[c][:].rearrange("p (a i) t -> p a t i", i=4),
+                u[c][:].rearrange("p t (a i) -> p a t i", i=4),
+                SILU,
+                bias=zero_bias[:],
+            )
+            nc.vector.quantize_mx(
+                out=z_codes[c][:].bitcast(FP8X4), scales=z_scales[c][:], in_=z[c][:].rearrange("p j t -> p (j t)")
+            )
+            acc = psum.tile([P, N // P, width], F32, name=f"acc{c}")
+            for b in range(N // P):
+                nc.tensor.matmul_mx(
+                    out=acc[:, b, :],
+                    lhsT=w2_codes[:, P * b : P * (b + 1)].bitcast(FP8X4),
+                    lhsT_scale=w2_scales[:, P * b : P * (b + 1)],
+                    rhs=z_codes[c][:].bitcast(FP8X4),
+                    rhs_scale=z_scales[c][:],
+                    start=True,
+                    stop=True,
+                )
+            result = keep.tile([P, N // P, width], F32, name=f"result{c}", align_bytes=64)
+            nc.scalar.copy(result[:], acc[:])
+            nc.sync.dma_start(out_rows[:, :, c0:c1], result[:])
+
+        later = range(1, len(CHUNKS))
+        for t in (0, 1):
+            first_tap(0, t)
+        later_taps(0, (0, 1))
+        for t in (2, 3):
+            for c in range(len(CHUNKS)):
+                first_tap(c, t)
+        for t in (0, 1):
+            for c in later:
+                first_tap(c, t)
+        later_taps(0, (2, 3))
+        nc.scalar.copy(
+            w2_bf[:].rearrange("p (a i) j -> p a j i", i=4),
+            w2_raw[:].rearrange("p j (a i) -> p a j i", i=4),
+        )
+        nc.vector.quantize_mx(
+            out=w2_codes[:].bitcast(FP8X4), scales=w2_scales[:], in_=w2_bf[:].rearrange("p c j -> p (c j)")
+        )
+        second_product(0)
+        for c in later:
+            later_taps(c, range(PACK))
+            second_product(c)

@@ -23,8 +23,13 @@ PACK = 4
 K_PASS = P * PACK
 PASSES = K // K_PASS
 QUADRANT = 32
-CHUNKS = ((0, 256), (256, 384), (384, 512))
-M_VECTOR = 84
+RUN = 4
+RUNS = P // RUN
+EARLY = 256
+LATE = 128
+LATE_CHUNKS = (S - EARLY) // LATE
+HELPED = ()
+RUNS_VECTOR = 22
 
 
 def tile_picked_dconv_silu_p_kernel(tc, x_words, x_scales, w1, w2, taps, offs, out):
@@ -38,142 +43,191 @@ def tile_picked_dconv_silu_p_kernel(tc, x_words, x_scales, w1, w2, taps, offs, o
         scales = keep.tile([P, PASSES, T], U8, name="scales", align_bytes=64)
         w1_raw = [keep.tile([P, PACK, H], F32, name=f"w1_raw{g}", align_bytes=64) for g in range(PASSES)]
         w2_raw = keep.tile([P, PACK, N], F32, name="w2_raw", align_bytes=64)
-        tap = keep.tile([P, PACK * D], F32, name="tap")
+        tap = [keep.tile([P, D], F32, name=f"tap{t}") for t in range(PACK)]
         zero_in = keep.tile([P, 1], F32, name="zero_in")
         zero_bias = keep.tile([P, 1], F32, name="zero_bias")
 
-        nc.vector.memset(scales[:].rearrange("p g c -> p (g c)").bitcast(I32), 0)
+        planes = scales[:].bitcast(I32)
+        nc.vector.memset(planes[:, 0, :], 0)
+        nc.gpsimd.memset(planes[:, 1, :], 0)
         nc.vector.memset(zero_in[:], 0.0)
         nc.scalar.activation(zero_bias[:], zero_in[:], SILU)
 
+        tap_rows = taps.rearrange("(a t r) d -> t a r d", t=PACK, r=RUN)
+        w2_rows = w2.rearrange("(a t r) c -> t a r c", t=PACK, r=RUN)
+        w1_rows = w1.rearrange("(g p j) c -> g p j c", j=PACK, p=P)
         nc.sync.dma_start(offsets[:], offs)
         nc.sync.dma_start(words[0][:].bitcast(I32), x_words[0].bitcast(I32))
-        nc.sync.dma_start(tap[:], taps.rearrange("(p t) d -> p (t d)", t=PACK))
+        nc.sync.dma_start(tap[0][:], tap_rows[0])
         for q in range(P // QUADRANT):
             nc.sync.dma_start(
-                scales[QUADRANT * q : QUADRANT * q + 4, :, :].bitcast(I32),
+                planes[QUADRANT * q : QUADRANT * q + 4, :, :],
                 x_scales[:, 4 * q : 4 * q + 4, :].rearrange("g r c -> r g c").bitcast(I32),
             )
-        nc.sync.dma_start(w1_raw[0][:], w1[0:K_PASS, :].rearrange("(p j) c -> p j c", j=PACK))
+        nc.sync.dma_start(w1_raw[0][:], w1_rows[0])
         nc.sync.dma_start(words[1][:].bitcast(I32), x_words[1].bitcast(I32))
-        nc.sync.dma_start(w1_raw[1][:], w1[K_PASS:K, :].rearrange("(p j) c -> p j c", j=PACK))
-        nc.sync.dma_start(w2_raw[:], w2.rearrange("(p j) c -> p j c", j=PACK))
+        nc.sync.dma_start(w1_raw[1][:], w1_rows[1])
+        for t in range(1, PACK):
+            nc.sync.dma_start(tap[t][:], tap_rows[t])
+        for t in range(PACK):
+            nc.sync.dma_start(w2_raw[:, t, :], w2_rows[t])
 
-        picked_words = [keep.tile([P, S], U16, name=f"picked_words{g}", align_bytes=64) for g in range(PASSES)]
+        picked_words = [keep.tile([P, S], U16, name="picked_words0", align_bytes=64)]
         picked_scales = [keep.tile([P, S], U8, name=f"picked_scales{g}", align_bytes=64) for g in range(PASSES)]
-        w1_bf = [keep.tile([P, PACK, P, PACK], BF16, name=f"w1_bf{g}", align_bytes=64) for g in range(PASSES)]
-        w1_codes = [[keep.tile([P, P], U32, name=f"w1_codes{g}_{t}", align_bytes=64) for t in range(PACK)] for g in range(PASSES)]
-        w1_scales = [[keep.tile([P, P], U8, name=f"w1_scales{g}_{t}", align_bytes=64) for t in range(PACK)] for g in range(PASSES)]
+        w1_codes = [keep.tile([P, PACK * P], U32, name=f"w1_codes{g}", align_bytes=64) for g in range(PASSES)]
+        w1_scales = [keep.tile([P, PACK * P], U8, name=f"w1_scales{g}", align_bytes=64) for g in range(PASSES)]
         h = [psum.tile([P, S], F32, name=f"h{t}") for t in range(PACK)]
 
-        def cast_w1(copy, g, m0, m1, t0, t1):
+        def cast_w1(copy, g, rounded, t0, a0, a1):
+            tiles = rounded.shape[1]
             copy(
-                w1_bf[g][:, t0:t1, m0:m1, :].rearrange("p t m j -> p m j t"),
-                w1_raw[g][:].rearrange("p j (m t) -> p m j t", t=PACK)[:, m0:m1, :, t0:t1],
+                rounded.rearrange("p t (a r) j -> p a t j r", r=RUN)[:, a0:a1],
+                w1_raw[g][:].rearrange("p j (a t r) -> p a t j r", t=PACK, r=RUN)[:, a0:a1, t0 : t0 + tiles],
             )
 
-        def first_product(g, t):
+        def first_product(g, rounded, t0):
+            t1 = t0 + rounded.shape[1]
             nc.vector.quantize_mx(
-                out=w1_codes[g][t][:].bitcast(FP8X4),
-                scales=w1_scales[g][t][:],
-                in_=w1_bf[g][:, t, :, :].rearrange("p m j -> p (m j)"),
+                out=w1_codes[g][:, P * t0 : P * t1].bitcast(FP8X4),
+                scales=w1_scales[g][:, P * t0 : P * t1],
+                in_=rounded.rearrange("p t m j -> p (t m j)"),
             )
-            nc.tensor.matmul_mx(
-                out=h[t][:],
-                lhsT=w1_codes[g][t][:].bitcast(FP8X4),
-                lhsT_scale=w1_scales[g][t][:],
-                rhs=picked_words[g][:].bitcast(FP4X4),
-                rhs_scale=picked_scales[g][:],
-                start=(g == 0),
-                stop=(g == PASSES - 1),
-            )
+            for t in range(t0, t1):
+                nc.tensor.matmul_mx(
+                    out=h[t][:],
+                    lhsT=w1_codes[g][:, P * t : P * (t + 1)].bitcast(FP8X4),
+                    lhsT_scale=w1_scales[g][:, P * t : P * (t + 1)],
+                    rhs=picked_words[g][:].bitcast(FP4X4),
+                    rhs_scale=picked_scales[g][:],
+                    start=(g == 0),
+                    stop=(g == PASSES - 1),
+                )
 
         nc.vector.tensor_copy(picked_words[0][:], words[0][:].indirect(offsets[:]))
-        nc.vector.tensor_copy(picked_scales[0][:], scales[:, 0, :].indirect(offsets[:]))
-        for t0 in (0, 2):
-            cast_w1(nc.scalar.copy, 0, 0, P, t0, t0 + 2)
-            first_product(0, t0)
-            first_product(0, t0 + 1)
-        nc.vector.tensor_copy(picked_scales[1][:], scales[:, 1, :].indirect(offsets[:]))
-        nc.vector.tensor_copy(picked_words[1][:], words[1][:].indirect(offsets[:]))
-        cast_w1(nc.vector.tensor_copy, 1, 0, M_VECTOR, 0, PACK)
-        cast_w1(nc.scalar.copy, 1, M_VECTOR, P, 0, PACK)
-        for t in range(PACK):
-            first_product(1, t)
+        for g in range(PASSES):
+            nc.vector.tensor_copy(picked_scales[g][:], scales[:, g, :].indirect(offsets[:]))
+        for t0, tag in ((0, "then_picked_words1"), (2, "w1_pair")):
+            pair = keep.tile([P, 2, P, PACK], BF16, name=f"w1_pair{t0}", tag=tag, align_bytes=64)
+            cast_w1(nc.scalar.copy, 0, pair[:], t0, 0, RUNS)
+            first_product(0, pair[:], t0)
+            if t0 == 0:
+                picked_words.append(
+                    keep.tile([P, S], U16, name="picked_words1", tag="then_picked_words1", align_bytes=64)
+                )
+                nc.vector.tensor_copy(picked_words[1][:], words[1][:].indirect(offsets[:]))
+        w1_last = keep.tile([P, PACK, P, PACK], BF16, name="w1_last", tag="then_w2_bf", align_bytes=64)
+        cast_w1(nc.vector.tensor_copy, 1, w1_last[:], 0, 0, RUNS_VECTOR)
+        cast_w1(nc.scalar.copy, 1, w1_last[:], 0, RUNS_VECTOR, RUNS)
+        for t0, t1 in ((0, 1), (1, 2), (2, 4)):
+            first_product(1, w1_last[:, t0:t1], t0)
 
-        u = [keep.tile([P, PACK, c1 - c0], F32, name=f"u{c0}", align_bytes=64) for c0, c1 in CHUNKS]
-        z = [keep.tile([P, c1 - c0, PACK], BF16, name=f"z{c0}", align_bytes=64) for c0, c1 in CHUNKS]
-        z_codes = [keep.tile([P, c1 - c0], U32, name=f"z_codes{c0}", align_bytes=64) for c0, c1 in CHUNKS]
-        z_scales = [keep.tile([P, c1 - c0], U8, name=f"z_scales{c0}", align_bytes=64) for c0, c1 in CHUNKS]
-        w2_bf = keep.tile([P, N, PACK], BF16, name="w2_bf", align_bytes=64)
+        u_early = keep.tile([P, PACK, EARLY], F32, name="u_early", align_bytes=64)
+        u_late = keep.tile([P, LATE_CHUNKS, PACK, LATE], F32, name="u_late", align_bytes=64)
+        second_tap = None
+        w2_bf = keep.tile([P, N, PACK], BF16, name="w2_bf", tag="then_w2_bf", align_bytes=64)
         w2_codes = keep.tile([P, N], U32, name="w2_codes", align_bytes=64)
         w2_scales = keep.tile([P, N], U8, name="w2_scales", align_bytes=64)
         out_rows = out.rearrange("(b p) j -> p b j", p=P)
 
-        def first_tap(c, t):
-            c0, c1 = CHUNKS[c]
-            nc.scalar.activation(u[c][:, t, :], h[t][:, c0:c1], COPY, scale=tap[:, D * t : D * t + 1])
+        def tap_of(t, d):
+            return tap[t][:, d : d + 1]
 
-        def later_taps(c, tiles):
-            c0, c1 = CHUNKS[c]
-            for d in range(1, D):
-                first = max(c0, d)
-                for t in tiles:
-                    nc.vector.scalar_tensor_tensor(
-                        out=u[c][:, t, first - c0 :],
-                        in0=h[t][:, first - d : c1 - d],
-                        scalar=tap[:, D * t + d : D * t + d + 1],
-                        in1=u[c][:, t, first - c0 :],
-                        op0=MULT,
-                        op1=ADD,
-                    )
+        def add_tap(u_rows, j0, t, d):
+            width = u_rows.shape[2]
+            first = max(j0, d)
+            nc.vector.scalar_tensor_tensor(
+                out=u_rows[:, t, first - j0 :],
+                in0=h[t][:, first - d : j0 + width - d],
+                scalar=tap_of(t, d),
+                in1=u_rows[:, t, first - j0 :],
+                op0=MULT,
+                op1=ADD,
+            )
 
-        def second_product(c):
-            c0, c1 = CHUNKS[c]
-            width = c1 - c0
+        def late_products(t):
+            targets = [u_late[:, :, t, :]]
+            if t in HELPED:
+                targets.append(second_tap[:, t, :, :])
+            for d, target in enumerate(targets):
+                source = h[t][:, EARLY - d : S - d].rearrange("p (c j) -> p c j", j=LATE)
+                nc.scalar.activation(target, source, COPY, scale=tap_of(t, d))
+            if t in HELPED:
+                nc.gpsimd.tensor_tensor(u_late[:, :, t, :], u_late[:, :, t, :], second_tap[:, t, :, :], ADD)
+
+        def quantized_z(u_rows, j0):
+            width = u_rows.shape[2]
+            z = keep.tile([P, width, PACK], BF16, name=f"z{j0}", align_bytes=64)
+            codes = keep.tile([P, width], U32, name=f"z_codes{j0}", align_bytes=64)
+            plane = keep.tile([P, width], U8, name=f"z_scales{j0}", align_bytes=64)
             nc.scalar.activation(
-                z[c][:].rearrange("p (a i) t -> p a t i", i=4),
-                u[c][:].rearrange("p t (a i) -> p a t i", i=4),
+                z[:].rearrange("p (a i) t -> p a t i", i=4),
+                u_rows.rearrange("p t (a i) -> p a t i", i=4),
                 SILU,
                 bias=zero_bias[:],
             )
-            nc.vector.quantize_mx(
-                out=z_codes[c][:].bitcast(FP8X4), scales=z_scales[c][:], in_=z[c][:].rearrange("p j t -> p (j t)")
-            )
-            acc = psum.tile([P, N // P, width], F32, name=f"acc{c}")
-            for b in range(N // P):
-                nc.tensor.matmul_mx(
-                    out=acc[:, b, :],
-                    lhsT=w2_codes[:, P * b : P * (b + 1)].bitcast(FP8X4),
-                    lhsT_scale=w2_scales[:, P * b : P * (b + 1)],
-                    rhs=z_codes[c][:].bitcast(FP8X4),
-                    rhs_scale=z_scales[c][:],
-                    start=True,
-                    stop=True,
-                )
-            result = keep.tile([P, N // P, width], F32, name=f"result{c}", align_bytes=64)
-            nc.scalar.copy(result[:], acc[:])
-            nc.sync.dma_start(out_rows[:, :, c0:c1], result[:])
+            nc.vector.quantize_mx(out=codes[:].bitcast(FP8X4), scales=plane[:], in_=z[:].rearrange("p j t -> p (j t)"))
+            return codes, plane
 
-        later = range(1, len(CHUNKS))
-        for t in (0, 1):
-            first_tap(0, t)
-        later_taps(0, (0, 1))
+        def second_product(acc, b, codes, plane):
+            nc.tensor.matmul_mx(
+                out=acc,
+                lhsT=w2_codes[:, P * b : P * (b + 1)].bitcast(FP8X4),
+                lhsT_scale=w2_scales[:, P * b : P * (b + 1)],
+                rhs=codes[:].bitcast(FP8X4),
+                rhs_scale=plane[:],
+                start=True,
+                stop=True,
+            )
+
+        def both_blocks(u_rows, j0):
+            codes, plane = quantized_z(u_rows, j0)
+            acc = psum.tile([P, N // P, u_rows.shape[2]], F32, name=f"acc{j0}")
+            for b in range(N // P):
+                second_product(acc[:, b, :], b, codes, plane)
+            return acc
+
+        def store_both(acc, j0, copy):
+            width = acc.shape[2]
+            result = keep.tile([P, N // P, width], F32, name=f"result{j0}", align_bytes=64)
+            copy(result[:], acc[:])
+            nc.sync.dma_start(out_rows[:, :, j0 : j0 + width], result[:])
+
+        def late_taps(c):
+            for d in range(1, D):
+                for t in (2, 0, 1, 3):
+                    if d > 1 or t not in HELPED:
+                        add_tap(u_late[:, c], EARLY + LATE * c, t, d)
+
+        nc.vector.tensor_scalar(u_early[:, 0, :], h[0][:, 0:EARLY], tap_of(0, 0), None, MULT)
+        nc.scalar.activation(u_early[:, 1, :], h[1][:, 0:EARLY], COPY, scale=tap_of(1, 0))
+        for d in range(1, D):
+            for t in (1, 0):
+                add_tap(u_early[:], 0, t, d)
         for t in (2, 3):
-            for c in range(len(CHUNKS)):
-                first_tap(c, t)
+            nc.scalar.activation(u_early[:, t, :], h[t][:, 0:EARLY], COPY, scale=tap_of(t, 0))
+            late_products(t)
         for t in (0, 1):
-            for c in later:
-                first_tap(c, t)
-        later_taps(0, (2, 3))
+            late_products(t)
         nc.scalar.copy(
-            w2_bf[:].rearrange("p (a i) j -> p a j i", i=4),
-            w2_raw[:].rearrange("p j (a i) -> p a j i", i=4),
+            w2_bf[:].rearrange("p (a i) j -> p a j i", i=4), w2_raw[:].rearrange("p j (a i) -> p a j i", i=4)
         )
+        for d in range(1, D):
+            for t in (2, 3):
+                add_tap(u_early[:], 0, t, d)
         nc.vector.quantize_mx(
             out=w2_codes[:].bitcast(FP8X4), scales=w2_scales[:], in_=w2_bf[:].rearrange("p c j -> p (c j)")
         )
-        second_product(0)
-        for c in later:
-            later_taps(c, range(PACK))
-            second_product(c)
+        acc_early = both_blocks(u_early[:], 0)
+        late_taps(0)
+        acc_late = both_blocks(u_late[:, 0], EARLY)
+        store_both(acc_early, 0, nc.scalar.copy)
+        late_taps(1)
+        j0 = EARLY + LATE
+        codes, plane = quantized_z(u_late[:, 1], j0)
+        store_both(acc_late, EARLY, nc.vector.tensor_copy)
+        for b, copy, queue in ((0, nc.vector.tensor_copy, nc.sync), (1, nc.scalar.copy, nc.scalar)):
+            acc = psum.tile([P, LATE], F32, name=f"acc_last{b}")
+            second_product(acc[:], b, codes, plane)
+            result = keep.tile([P, LATE], F32, name=f"result_last{b}", align_bytes=64)
+            copy(result[:], acc[:])
+            queue.dma_start(out_rows[:, b, j0:S], result[:])

@@ -23,13 +23,10 @@ PACK = 4
 K_PASS = P * PACK
 PASSES = K // K_PASS
 QUADRANT = 32
-RUN = 4
-RUNS = P // RUN
 EARLY = 256
 LATE = 128
 LATE_CHUNKS = (S - EARLY) // LATE
-HELPED = ()
-RUNS_VECTOR = 22
+M_VECTOR = 84
 
 
 def tile_picked_dconv_silu_p_kernel(tc, x_words, x_scales, w1, w2, taps, offs, out):
@@ -43,94 +40,78 @@ def tile_picked_dconv_silu_p_kernel(tc, x_words, x_scales, w1, w2, taps, offs, o
         scales = keep.tile([P, PASSES, T], U8, name="scales", align_bytes=64)
         w1_raw = [keep.tile([P, PACK, H], F32, name=f"w1_raw{g}", align_bytes=64) for g in range(PASSES)]
         w2_raw = keep.tile([P, PACK, N], F32, name="w2_raw", align_bytes=64)
-        tap = [keep.tile([P, D], F32, name=f"tap{t}") for t in range(PACK)]
+        tap = keep.tile([P, PACK * D], F32, name="tap")
         zero_in = keep.tile([P, 1], F32, name="zero_in")
         zero_bias = keep.tile([P, 1], F32, name="zero_bias")
 
-        planes = scales[:].bitcast(I32)
-        nc.vector.memset(planes[:, 0, :], 0)
-        nc.gpsimd.memset(planes[:, 1, :], 0)
+        nc.vector.memset(scales[:].rearrange("p g c -> p (g c)").bitcast(I32), 0)
         nc.vector.memset(zero_in[:], 0.0)
         nc.scalar.activation(zero_bias[:], zero_in[:], SILU)
 
-        tap_rows = taps.rearrange("(a t r) d -> t a r d", t=PACK, r=RUN)
-        w2_rows = w2.rearrange("(a t r) c -> t a r c", t=PACK, r=RUN)
-        w1_rows = w1.rearrange("(g p j) c -> g p j c", j=PACK, p=P)
-        nc.sync.dma_start(offsets[:], offs)
         nc.sync.dma_start(words[0][:].bitcast(I32), x_words[0].bitcast(I32))
-        nc.sync.dma_start(tap[0][:], tap_rows[0])
+        nc.sync.dma_start(offsets[:], offs)
+        nc.sync.dma_start(tap[:], taps.rearrange("(p t) d -> p (t d)", t=PACK))
         for q in range(P // QUADRANT):
             nc.sync.dma_start(
-                planes[QUADRANT * q : QUADRANT * q + 4, :, :],
+                scales[QUADRANT * q : QUADRANT * q + 4, :, :].bitcast(I32),
                 x_scales[:, 4 * q : 4 * q + 4, :].rearrange("g r c -> r g c").bitcast(I32),
             )
-        nc.sync.dma_start(w1_raw[0][:], w1_rows[0])
+        nc.sync.dma_start(w1_raw[0][:], w1[0:K_PASS, :].rearrange("(p j) c -> p j c", j=PACK))
         nc.sync.dma_start(words[1][:].bitcast(I32), x_words[1].bitcast(I32))
-        nc.sync.dma_start(w1_raw[1][:], w1_rows[1])
-        for t in range(1, PACK):
-            nc.sync.dma_start(tap[t][:], tap_rows[t])
-        for t in range(PACK):
-            nc.sync.dma_start(w2_raw[:, t, :], w2_rows[t])
+        nc.sync.dma_start(w1_raw[1][:], w1[K_PASS:K, :].rearrange("(p j) c -> p j c", j=PACK))
+        nc.sync.dma_start(w2_raw[:], w2.rearrange("(p j) c -> p j c", j=PACK))
 
-        picked_words = [keep.tile([P, S], U16, name="picked_words0", align_bytes=64)]
+        picked_words = [keep.tile([P, S], U16, name=f"picked_words{g}", align_bytes=64) for g in range(PASSES)]
         picked_scales = [keep.tile([P, S], U8, name=f"picked_scales{g}", align_bytes=64) for g in range(PASSES)]
-        w1_codes = [keep.tile([P, PACK * P], U32, name=f"w1_codes{g}", align_bytes=64) for g in range(PASSES)]
-        w1_scales = [keep.tile([P, PACK * P], U8, name=f"w1_scales{g}", align_bytes=64) for g in range(PASSES)]
+        w1_bf = [keep.tile([P, PACK, P, PACK], BF16, name=f"w1_bf{g}", align_bytes=64) for g in range(PASSES)]
+        w1_codes = [[keep.tile([P, P], U32, name=f"w1_codes{g}_{t}", align_bytes=64) for t in range(PACK)] for g in range(PASSES)]
+        w1_scales = [[keep.tile([P, P], U8, name=f"w1_scales{g}_{t}", align_bytes=64) for t in range(PACK)] for g in range(PASSES)]
         h = [psum.tile([P, S], F32, name=f"h{t}") for t in range(PACK)]
 
-        def cast_w1(copy, g, rounded, t0, a0, a1):
-            tiles = rounded.shape[1]
+        def cast_w1(copy, g, m0, m1, t0, t1):
             copy(
-                rounded.rearrange("p t (a r) j -> p a t j r", r=RUN)[:, a0:a1],
-                w1_raw[g][:].rearrange("p j (a t r) -> p a t j r", t=PACK, r=RUN)[:, a0:a1, t0 : t0 + tiles],
+                w1_bf[g][:, t0:t1, m0:m1, :].rearrange("p t m j -> p m j t"),
+                w1_raw[g][:].rearrange("p j (m t) -> p m j t", t=PACK)[:, m0:m1, :, t0:t1],
             )
 
-        def first_product(g, rounded, t0):
-            t1 = t0 + rounded.shape[1]
+        def first_product(g, t):
             nc.vector.quantize_mx(
-                out=w1_codes[g][:, P * t0 : P * t1].bitcast(FP8X4),
-                scales=w1_scales[g][:, P * t0 : P * t1],
-                in_=rounded.rearrange("p t m j -> p (t m j)"),
+                out=w1_codes[g][t][:].bitcast(FP8X4),
+                scales=w1_scales[g][t][:],
+                in_=w1_bf[g][:, t, :, :].rearrange("p m j -> p (m j)"),
             )
-            for t in range(t0, t1):
-                nc.tensor.matmul_mx(
-                    out=h[t][:],
-                    lhsT=w1_codes[g][:, P * t : P * (t + 1)].bitcast(FP8X4),
-                    lhsT_scale=w1_scales[g][:, P * t : P * (t + 1)],
-                    rhs=picked_words[g][:].bitcast(FP4X4),
-                    rhs_scale=picked_scales[g][:],
-                    start=(g == 0),
-                    stop=(g == PASSES - 1),
-                )
+            nc.tensor.matmul_mx(
+                out=h[t][:],
+                lhsT=w1_codes[g][t][:].bitcast(FP8X4),
+                lhsT_scale=w1_scales[g][t][:],
+                rhs=picked_words[g][:].bitcast(FP4X4),
+                rhs_scale=picked_scales[g][:],
+                start=(g == 0),
+                stop=(g == PASSES - 1),
+            )
 
         nc.vector.tensor_copy(picked_words[0][:], words[0][:].indirect(offsets[:]))
-        for g in range(PASSES):
-            nc.vector.tensor_copy(picked_scales[g][:], scales[:, g, :].indirect(offsets[:]))
-        for t0, tag in ((0, "then_picked_words1"), (2, "w1_pair")):
-            pair = keep.tile([P, 2, P, PACK], BF16, name=f"w1_pair{t0}", tag=tag, align_bytes=64)
-            cast_w1(nc.scalar.copy, 0, pair[:], t0, 0, RUNS)
-            first_product(0, pair[:], t0)
-            if t0 == 0:
-                picked_words.append(
-                    keep.tile([P, S], U16, name="picked_words1", tag="then_picked_words1", align_bytes=64)
-                )
-                nc.vector.tensor_copy(picked_words[1][:], words[1][:].indirect(offsets[:]))
-        w1_last = keep.tile([P, PACK, P, PACK], BF16, name="w1_last", tag="then_w2_bf", align_bytes=64)
-        cast_w1(nc.vector.tensor_copy, 1, w1_last[:], 0, 0, RUNS_VECTOR)
-        cast_w1(nc.scalar.copy, 1, w1_last[:], 0, RUNS_VECTOR, RUNS)
-        for t0, t1 in ((0, 1), (1, 2), (2, 4)):
-            first_product(1, w1_last[:, t0:t1], t0)
+        nc.vector.tensor_copy(picked_scales[0][:], scales[:, 0, :].indirect(offsets[:]))
+        for t0 in (0, 2):
+            cast_w1(nc.scalar.copy, 0, 0, P, t0, t0 + 2)
+            first_product(0, t0)
+            first_product(0, t0 + 1)
+        nc.vector.tensor_copy(picked_scales[1][:], scales[:, 1, :].indirect(offsets[:]))
+        nc.vector.tensor_copy(picked_words[1][:], words[1][:].indirect(offsets[:]))
+        cast_w1(nc.vector.tensor_copy, 1, 0, M_VECTOR, 0, PACK)
+        cast_w1(nc.scalar.copy, 1, M_VECTOR, P, 0, PACK)
+        for t in range(PACK):
+            first_product(1, t)
 
         u_early = keep.tile([P, PACK, EARLY], F32, name="u_early", align_bytes=64)
         u_late = keep.tile([P, LATE_CHUNKS, PACK, LATE], F32, name="u_late", align_bytes=64)
-        second_tap = None
-        w2_bf = keep.tile([P, N, PACK], BF16, name="w2_bf", tag="then_w2_bf", align_bytes=64)
+        w2_bf = keep.tile([P, N, PACK], BF16, name="w2_bf", align_bytes=64)
         w2_codes = keep.tile([P, N], U32, name="w2_codes", align_bytes=64)
         w2_scales = keep.tile([P, N], U8, name="w2_scales", align_bytes=64)
         out_rows = out.rearrange("(b p) j -> p b j", p=P)
 
         def tap_of(t, d):
-            return tap[t][:, d : d + 1]
+            return tap[:, D * t + d : D * t + d + 1]
 
         def add_tap(u_rows, j0, t, d):
             width = u_rows.shape[2]
@@ -145,14 +126,8 @@ def tile_picked_dconv_silu_p_kernel(tc, x_words, x_scales, w1, w2, taps, offs, o
             )
 
         def late_products(t):
-            targets = [u_late[:, :, t, :]]
-            if t in HELPED:
-                targets.append(second_tap[:, t, :, :])
-            for d, target in enumerate(targets):
-                source = h[t][:, EARLY - d : S - d].rearrange("p (c j) -> p c j", j=LATE)
-                nc.scalar.activation(target, source, COPY, scale=tap_of(t, d))
-            if t in HELPED:
-                nc.gpsimd.tensor_tensor(u_late[:, :, t, :], u_late[:, :, t, :], second_tap[:, t, :, :], ADD)
+            source = h[t][:, EARLY:S].rearrange("p (c j) -> p c j", j=LATE)
+            nc.scalar.activation(u_late[:, :, t, :], source, COPY, scale=tap_of(t, 0))
 
         def quantized_z(u_rows, j0):
             width = u_rows.shape[2]
@@ -194,9 +169,8 @@ def tile_picked_dconv_silu_p_kernel(tc, x_words, x_scales, w1, w2, taps, offs, o
 
         def late_taps(c):
             for d in range(1, D):
-                for t in (2, 0, 1, 3):
-                    if d > 1 or t not in HELPED:
-                        add_tap(u_late[:, c], EARLY + LATE * c, t, d)
+                for t in (2, 3, 0, 1):
+                    add_tap(u_late[:, c], EARLY + LATE * c, t, d)
 
         nc.vector.tensor_scalar(u_early[:, 0, :], h[0][:, 0:EARLY], tap_of(0, 0), None, MULT)
         nc.scalar.activation(u_early[:, 1, :], h[1][:, 0:EARLY], COPY, scale=tap_of(1, 0))
@@ -225,9 +199,9 @@ def tile_picked_dconv_silu_p_kernel(tc, x_words, x_scales, w1, w2, taps, offs, o
         j0 = EARLY + LATE
         codes, plane = quantized_z(u_late[:, 1], j0)
         store_both(acc_late, EARLY, nc.vector.tensor_copy)
-        for b, copy, queue in ((0, nc.vector.tensor_copy, nc.sync), (1, nc.scalar.copy, nc.scalar)):
+        for b, copy in ((0, nc.vector.tensor_copy), (1, nc.scalar.copy)):
             acc = psum.tile([P, LATE], F32, name=f"acc_last{b}")
             second_product(acc[:], b, codes, plane)
             result = keep.tile([P, LATE], F32, name=f"result_last{b}", align_bytes=64)
             copy(result[:], acc[:])
-            queue.dma_start(out_rows[:, b, j0:S], result[:])
+            nc.sync.dma_start(out_rows[:, b, j0:S], result[:])

@@ -104,8 +104,8 @@ def tile_picked_dconv_silu_p_kernel(tc, x_words, x_scales, w1, w2, taps, offs, o
             first_product(1, t)
 
         u_early = keep.tile([P, PACK, EARLY], F32, name="u_early", align_bytes=64)
-        u_late = keep.tile([P, LATE_CHUNKS, PACK, LATE], F32, name="u_late", align_bytes=64)
-        w2_bf = keep.tile([P, N, PACK], BF16, name="w2_bf", align_bytes=64)
+        u_late = keep.tile([P, LATE_CHUNKS, PACK, LATE], F32, name="u_late", tag="shared", align_bytes=64)
+        w2_bf = keep.tile([P, N, PACK], BF16, name="w2_bf", tag="w2_bf", align_bytes=64)
         w2_codes = keep.tile([P, N], U32, name="w2_codes", align_bytes=64)
         w2_scales = keep.tile([P, N], U8, name="w2_scales", align_bytes=64)
         out_rows = out.rearrange("(b p) j -> p b j", p=P)
@@ -125,21 +125,36 @@ def tile_picked_dconv_silu_p_kernel(tc, x_words, x_scales, w1, w2, taps, offs, o
                 op1=ADD,
             )
 
-        def late_products(t):
-            source = h[t][:, EARLY:S].rearrange("p (c j) -> p c j", j=LATE)
-            nc.scalar.activation(u_late[:, :, t, :], source, COPY, scale=tap_of(t, 0))
+        def late_columns(t, d):
+            return h[t][:, EARLY - d : S - d].rearrange("p (c j) -> p c j", j=LATE)
 
-        def quantized_z(u_rows, j0):
-            width = u_rows.shape[2]
-            z = keep.tile([P, width, PACK], BF16, name=f"z{j0}", align_bytes=64)
-            codes = keep.tile([P, width], U32, name=f"z_codes{j0}", align_bytes=64)
-            plane = keep.tile([P, width], U8, name=f"z_scales{j0}", align_bytes=64)
+        def late_products(t):
+            nc.scalar.activation(u_late[:, :, t, :], late_columns(t, 0), COPY, scale=tap_of(t, 0))
+
+        def side_product(t, c0):
+            source = late_columns(t, D - 1)[:, c0:, :]
+            nc.scalar.activation(side[:, c0:, t, :], source, COPY, scale=tap_of(t, D - 1))
+
+        def add_side(t0, c0):
+            sums = u_late[:, c0:, t0 : t0 + 2, :]
+            nc.gpsimd.tensor_tensor(sums, sums, side[:, c0:, t0 : t0 + 2, :], ADD)
+
+        def silu_into(z, u_rows):
             nc.scalar.activation(
-                z[:].rearrange("p (a i) t -> p a t i", i=4),
+                z.rearrange("p (a i) t -> p a t i", i=4),
                 u_rows.rearrange("p t (a i) -> p a t i", i=4),
                 SILU,
                 bias=zero_bias[:],
             )
+
+        def silu_z(u_rows, j0, tag):
+            z = keep.tile([P, u_rows.shape[2], PACK], BF16, name=f"z{j0}", tag=tag, align_bytes=64)
+            silu_into(z[:], u_rows)
+            return z
+
+        def quantized(z, j0):
+            codes = keep.tile([P, z.shape[1]], U32, name=f"z_codes{j0}", align_bytes=64)
+            plane = keep.tile([P, z.shape[1]], U8, name=f"z_scales{j0}", align_bytes=64)
             nc.vector.quantize_mx(out=codes[:].bitcast(FP8X4), scales=plane[:], in_=z[:].rearrange("p j t -> p (j t)"))
             return codes, plane
 
@@ -154,51 +169,64 @@ def tile_picked_dconv_silu_p_kernel(tc, x_words, x_scales, w1, w2, taps, offs, o
                 stop=True,
             )
 
-        def both_blocks(u_rows, j0):
-            codes, plane = quantized_z(u_rows, j0)
-            acc = psum.tile([P, N // P, u_rows.shape[2]], F32, name=f"acc{j0}")
+        def both_blocks(z, j0):
+            codes, plane = quantized(z, j0)
+            acc = psum.tile([P, N // P, z.shape[1]], F32, name=f"acc{j0}")
             for b in range(N // P):
                 second_product(acc[:, b, :], b, codes, plane)
             return acc
 
-        def store_both(acc, j0, copy):
+        def store_both(acc, j0, tag, copy):
             width = acc.shape[2]
-            result = keep.tile([P, N // P, width], F32, name=f"result{j0}", align_bytes=64)
+            result = keep.tile([P, N // P, width], F32, name=f"result{j0}", tag=tag, align_bytes=64)
             copy(result[:], acc[:])
             nc.sync.dma_start(out_rows[:, :, j0 : j0 + width], result[:])
 
-        def late_taps(c):
-            for d in range(1, D):
-                for t in (2, 3, 0, 1):
-                    add_tap(u_late[:, c], EARLY + LATE * c, t, d)
-
+        nc.scalar.copy(
+            w2_bf[:].rearrange("p (a i) j -> p a j i", i=4), w2_raw[:].rearrange("p j (a i) -> p a j i", i=4)
+        )
         nc.vector.tensor_scalar(u_early[:, 0, :], h[0][:, 0:EARLY], tap_of(0, 0), None, MULT)
         nc.scalar.activation(u_early[:, 1, :], h[1][:, 0:EARLY], COPY, scale=tap_of(1, 0))
+        nc.vector.quantize_mx(
+            out=w2_codes[:].bitcast(FP8X4), scales=w2_scales[:], in_=w2_bf[:].rearrange("p c j -> p (c j)")
+        )
+        side = keep.tile([P, LATE_CHUNKS, PACK, LATE], F32, name="side", tag="w2_bf", align_bytes=64)
         for d in range(1, D):
             for t in (1, 0):
                 add_tap(u_early[:], 0, t, d)
         for t in (2, 3):
             nc.scalar.activation(u_early[:, t, :], h[t][:, 0:EARLY], COPY, scale=tap_of(t, 0))
             late_products(t)
+        for t in (2, 3):
+            side_product(t, 0)
+        add_side(2, 0)
         for t in (0, 1):
             late_products(t)
-        nc.scalar.copy(
-            w2_bf[:].rearrange("p (a i) j -> p a j i", i=4), w2_raw[:].rearrange("p j (a i) -> p a j i", i=4)
-        )
-        for d in range(1, D):
+            side_product(t, 1)
+        add_side(0, 1)
+        for d in range(1, D - 1):
             for t in (2, 3):
                 add_tap(u_early[:], 0, t, d)
-        nc.vector.quantize_mx(
-            out=w2_codes[:].bitcast(FP8X4), scales=w2_scales[:], in_=w2_bf[:].rearrange("p c j -> p (c j)")
-        )
-        acc_early = both_blocks(u_early[:], 0)
-        late_taps(0)
-        acc_late = both_blocks(u_late[:, 0], EARLY)
-        store_both(acc_early, 0, nc.scalar.copy)
-        late_taps(1)
+        z_early = keep.tile([P, EARLY, PACK], BF16, name="z_early", align_bytes=64)
+        for j0 in range(0, EARLY, LATE):
+            for t in (2, 3):
+                add_tap(u_early[:, :, j0 : j0 + LATE], j0, t, D - 1)
+            silu_into(z_early[:, j0 : j0 + LATE, :], u_early[:, :, j0 : j0 + LATE])
+        acc_early = both_blocks(z_early, 0)
+        z_late = []
+        for c in range(LATE_CHUNKS):
+            for d in range(1, D - 1):
+                for t in (0, 1, 2, 3):
+                    add_tap(u_late[:, c], EARLY + LATE * c, t, d)
+            if c == 0:
+                for t in (0, 1):
+                    add_tap(u_late[:, c], EARLY, t, D - 1)
+            z_late.append(silu_z(u_late[:, c], EARLY + LATE * c, f"z_late{c}"))
         j0 = EARLY + LATE
-        codes, plane = quantized_z(u_late[:, 1], j0)
-        store_both(acc_late, EARLY, nc.vector.tensor_copy)
+        acc_mid = both_blocks(z_late[0], EARLY)
+        store_both(acc_early, 0, "early_result", nc.vector.tensor_copy)
+        codes, plane = quantized(z_late[1], j0)
+        store_both(acc_mid, EARLY, "shared", nc.scalar.copy)
         for b, copy in ((0, nc.vector.tensor_copy), (1, nc.scalar.copy)):
             acc = psum.tile([P, LATE], F32, name=f"acc_last{b}")
             second_product(acc[:], b, codes, plane)

@@ -23,10 +23,10 @@ PACK = 4
 K_PASS = P * PACK
 PASSES = K // K_PASS
 QUADRANT = 32
-EARLY = 256
-LATE = 128
-LATE_CHUNKS = (S - EARLY) // LATE
-M_VECTOR = 84
+HALF = 256
+CHUNK = 128
+M_VECTOR_0 = 56
+M_VECTOR_1 = 84
 
 
 def tile_picked_dconv_silu_p_kernel(tc, x_words, x_scales, w1, w2, taps, offs, out):
@@ -43,69 +43,87 @@ def tile_picked_dconv_silu_p_kernel(tc, x_words, x_scales, w1, w2, taps, offs, o
         tap = keep.tile([P, PACK * D], F32, name="tap")
         zero_in = keep.tile([P, 1], F32, name="zero_in")
         zero_bias = keep.tile([P, 1], F32, name="zero_bias")
+        u = keep.tile([P, PACK, S], F32, name="u", align_bytes=64)
 
         nc.vector.memset(scales[:].rearrange("p g c -> p (g c)").bitcast(I32), 0)
         nc.vector.memset(zero_in[:], 0.0)
+        nc.vector.memset(u[:, :, 0 : D - 1], 0.0)
         nc.scalar.activation(zero_bias[:], zero_in[:], SILU)
 
         nc.sync.dma_start(words[0][:].bitcast(I32), x_words[0].bitcast(I32))
         nc.sync.dma_start(offsets[:], offs)
-        nc.sync.dma_start(tap[:], taps.rearrange("(p t) d -> p (t d)", t=PACK))
-        for q in range(P // QUADRANT):
+        nc.sync.dma_start(words[1][:].bitcast(I32), x_words[1].bitcast(I32))
+        for r in range(4):
             nc.sync.dma_start(
-                scales[QUADRANT * q : QUADRANT * q + 4, :, :].bitcast(I32),
-                x_scales[:, 4 * q : 4 * q + 4, :].rearrange("g r c -> r g c").bitcast(I32),
+                scales[r:P:QUADRANT, :, :].bitcast(I32),
+                x_scales[:, r:16:4, :].rearrange("g q c -> q g c").bitcast(I32),
             )
         nc.sync.dma_start(w1_raw[0][:], w1[0:K_PASS, :].rearrange("(p j) c -> p j c", j=PACK))
-        nc.sync.dma_start(words[1][:].bitcast(I32), x_words[1].bitcast(I32))
         nc.sync.dma_start(w1_raw[1][:], w1[K_PASS:K, :].rearrange("(p j) c -> p j c", j=PACK))
+        nc.sync.dma_start(tap[:], taps.rearrange("(p t) d -> p (t d)", t=PACK))
         nc.sync.dma_start(w2_raw[:], w2.rearrange("(p j) c -> p j c", j=PACK))
 
-        picked_words = [keep.tile([P, S], U16, name=f"picked_words{g}", align_bytes=64) for g in range(PASSES)]
+        picked_words0 = keep.tile([P, S], U16, name="picked_words0", align_bytes=64)
+        picked_early1 = keep.tile([P, HALF], U16, name="picked_early1", tag="picked_early1", align_bytes=64)
         picked_scales = [keep.tile([P, S], U8, name=f"picked_scales{g}", align_bytes=64) for g in range(PASSES)]
-        w1_bf = [keep.tile([P, PACK, P, PACK], BF16, name=f"w1_bf{g}", align_bytes=64) for g in range(PASSES)]
+        w1_bf = [
+            [keep.tile([P, 2, P, PACK], BF16, name=f"w1_bf{g}_{a}", tag=f"w1_bf{g}_{a}", align_bytes=64) for a in range(2)]
+            for g in range(PASSES)
+        ]
         w1_codes = [[keep.tile([P, P], U32, name=f"w1_codes{g}_{t}", align_bytes=64) for t in range(PACK)] for g in range(PASSES)]
         w1_scales = [[keep.tile([P, P], U8, name=f"w1_scales{g}_{t}", align_bytes=64) for t in range(PACK)] for g in range(PASSES)]
-        h = [psum.tile([P, S], F32, name=f"h{t}") for t in range(PACK)]
+        h = [[psum.tile([P, HALF], F32, name=f"h{half}_{t}", tag=f"bank{half}_{t}") for t in range(PACK)] for half in range(2)]
 
-        def cast_w1(copy, g, m0, m1, t0, t1):
+        def cast_w1(copy, g, a, m0, m1):
             copy(
-                w1_bf[g][:, t0:t1, m0:m1, :].rearrange("p t m j -> p m j t"),
-                w1_raw[g][:].rearrange("p j (m t) -> p m j t", t=PACK)[:, m0:m1, :, t0:t1],
+                w1_bf[g][a][:, :, m0:m1, :].rearrange("p t m j -> p m j t"),
+                w1_raw[g][:].rearrange("p j (m t) -> p m j t", t=PACK)[:, m0:m1, :, 2 * a : 2 * a + 2],
             )
 
-        def first_product(g, t):
+        def quantize_w1(g, t):
             nc.vector.quantize_mx(
                 out=w1_codes[g][t][:].bitcast(FP8X4),
                 scales=w1_scales[g][t][:],
-                in_=w1_bf[g][:, t, :, :].rearrange("p m j -> p (m j)"),
+                in_=w1_bf[g][t // 2][:, t % 2, :, :].rearrange("p m j -> p (m j)"),
             )
+
+        def first_product(g, t, half, moving, opens):
             nc.tensor.matmul_mx(
-                out=h[t][:],
+                out=h[half][t][:],
                 lhsT=w1_codes[g][t][:].bitcast(FP8X4),
                 lhsT_scale=w1_scales[g][t][:],
-                rhs=picked_words[g][:].bitcast(FP4X4),
-                rhs_scale=picked_scales[g][:],
-                start=(g == 0),
-                stop=(g == PASSES - 1),
+                rhs=moving.bitcast(FP4X4),
+                rhs_scale=picked_scales[g][:, HALF * half : HALF * (half + 1)],
+                start=opens,
+                stop=not opens,
             )
 
-        nc.vector.tensor_copy(picked_words[0][:], words[0][:].indirect(offsets[:]))
-        nc.vector.tensor_copy(picked_scales[0][:], scales[:, 0, :].indirect(offsets[:]))
-        for t0 in (0, 2):
-            cast_w1(nc.scalar.copy, 0, 0, P, t0, t0 + 2)
-            first_product(0, t0)
-            first_product(0, t0 + 1)
-        nc.vector.tensor_copy(picked_scales[1][:], scales[:, 1, :].indirect(offsets[:]))
-        nc.vector.tensor_copy(picked_words[1][:], words[1][:].indirect(offsets[:]))
-        cast_w1(nc.vector.tensor_copy, 1, 0, M_VECTOR, 0, PACK)
-        cast_w1(nc.scalar.copy, 1, M_VECTOR, P, 0, PACK)
+        nc.vector.tensor_copy(picked_words0[:], words[0][:].indirect(offsets[:]))
+        nc.vector.tensor_copy(picked_early1[:], words[1][:].indirect(offsets[:, 0 : HALF // 16]))
+        for g in range(PASSES):
+            nc.vector.tensor_copy(picked_scales[g][:], scales[:, g, :].indirect(offsets[:]))
+        cast_w1(nc.scalar.copy, 0, 0, 0, P)
+        cast_w1(nc.vector.tensor_copy, 0, 1, 0, M_VECTOR_0)
+        cast_w1(nc.scalar.copy, 0, 1, M_VECTOR_0, P)
         for t in range(PACK):
-            first_product(1, t)
+            quantize_w1(0, t)
+            first_product(0, t, 0, picked_words0[:, 0:HALF], True)
+        for a in range(2):
+            cast_w1(nc.vector.tensor_copy, 1, a, 0, M_VECTOR_1)
+            cast_w1(nc.scalar.copy, 1, a, M_VECTOR_1, P)
+        for t in range(PACK):
+            quantize_w1(1, t)
+            first_product(1, t, 0, picked_early1[:], False)
+        picked_late1 = keep.tile([P, HALF], U16, name="picked_late1", tag="w1_bf1_0", align_bytes=64)
+        nc.vector.tensor_copy(picked_late1[:], words[1][:].indirect(offsets[:, HALF // 16 : S // 16]))
+        for t in range(PACK):
+            first_product(1, t, 1, picked_late1[:], True)
+            first_product(0, t, 1, picked_words0[:, HALF:S], False)
 
-        u_early = keep.tile([P, PACK, EARLY], F32, name="u_early", align_bytes=64)
-        u_late = keep.tile([P, LATE_CHUNKS, PACK, LATE], F32, name="u_late", tag="shared", align_bytes=64)
-        w2_bf = keep.tile([P, N, PACK], BF16, name="w2_bf", tag="w2_bf", align_bytes=64)
+        w2_bf = [
+            keep.tile([P, P, PACK], BF16, name=f"w2_bf{b}", tag=tag, align_bytes=64)
+            for b, tag in enumerate(("w2_bf0", "picked_early1"))
+        ]
         w2_codes = keep.tile([P, N], U32, name="w2_codes", align_bytes=64)
         w2_scales = keep.tile([P, N], U8, name="w2_scales", align_bytes=64)
         out_rows = out.rearrange("(b p) j -> p b j", p=P)
@@ -113,44 +131,36 @@ def tile_picked_dconv_silu_p_kernel(tc, x_words, x_scales, w1, w2, taps, offs, o
         def tap_of(t, d):
             return tap[:, D * t + d : D * t + d + 1]
 
-        def add_tap(u_rows, j0, t, d):
-            width = u_rows.shape[2]
-            first = max(j0, d)
+        def first_tap(half, t):
+            j0 = HALF * half + D - 1
+            j1 = min(j0 + HALF, S)
+            nc.scalar.activation(u[:, t, j0:j1], h[half][t][:, 0 : j1 - j0], COPY, scale=tap_of(t, D - 1))
+
+        def add_tap(half, t, d, j0, j1):
+            base = HALF * half + d
             nc.vector.scalar_tensor_tensor(
-                out=u_rows[:, t, first - j0 :],
-                in0=h[t][:, first - d : j0 + width - d],
+                out=u[:, t, j0:j1],
+                in0=h[half][t][:, j0 - base : j1 - base],
                 scalar=tap_of(t, d),
-                in1=u_rows[:, t, first - j0 :],
+                in1=u[:, t, j0:j1],
                 op0=MULT,
                 op1=ADD,
             )
 
-        def late_columns(t, d):
-            return h[t][:, EARLY - d : S - d].rearrange("p (c j) -> p c j", j=LATE)
-
-        def late_products(t):
-            nc.scalar.activation(u_late[:, :, t, :], late_columns(t, 0), COPY, scale=tap_of(t, 0))
-
         def side_product(t, c0):
-            source = late_columns(t, D - 1)[:, c0:, :]
-            nc.scalar.activation(side[:, c0:, t, :], source, COPY, scale=tap_of(t, D - 1))
+            nc.scalar.activation(side[:, t, c0:HALF], h[1][t][:, c0:HALF], COPY, scale=tap_of(t, 0))
 
-        def add_side(t0, c0):
-            sums = u_late[:, c0:, t0 : t0 + 2, :]
-            nc.gpsimd.tensor_tensor(sums, sums, side[:, c0:, t0 : t0 + 2, :], ADD)
+        def add_side(t0, t1, c0):
+            sums = u[:, t0:t1, HALF + c0 : HALF + c0 + CHUNK]
+            nc.gpsimd.tensor_tensor(sums, sums, side[:, t0:t1, c0 : c0 + CHUNK], ADD)
 
-        def silu_into(z, u_rows):
+        def silu_into(z, j0):
             nc.scalar.activation(
                 z.rearrange("p (a i) t -> p a t i", i=4),
-                u_rows.rearrange("p t (a i) -> p a t i", i=4),
+                u[:, :, j0 : j0 + CHUNK].rearrange("p t (a i) -> p a t i", i=4),
                 SILU,
                 bias=zero_bias[:],
             )
-
-        def silu_z(u_rows, j0, tag):
-            z = keep.tile([P, u_rows.shape[2], PACK], BF16, name=f"z{j0}", tag=tag, align_bytes=64)
-            silu_into(z[:], u_rows)
-            return z
 
         def quantized(z, j0):
             codes = keep.tile([P, z.shape[1]], U32, name=f"z_codes{j0}", align_bytes=64)
@@ -169,67 +179,76 @@ def tile_picked_dconv_silu_p_kernel(tc, x_words, x_scales, w1, w2, taps, offs, o
                 stop=True,
             )
 
-        def both_blocks(z, j0):
+        def both_blocks(z, j0, bank):
             codes, plane = quantized(z, j0)
-            acc = psum.tile([P, N // P, z.shape[1]], F32, name=f"acc{j0}")
+            acc = psum.tile([P, N // P, z.shape[1]], F32, name=f"acc{j0}", tag=bank)
             for b in range(N // P):
                 second_product(acc[:, b, :], b, codes, plane)
             return acc
 
-        def store_both(acc, j0, tag, copy):
-            width = acc.shape[2]
-            result = keep.tile([P, N // P, width], F32, name=f"result{j0}", tag=tag, align_bytes=64)
-            copy(result[:], acc[:])
-            nc.sync.dma_start(out_rows[:, :, j0 : j0 + width], result[:])
+        def store_both(acc, j0, result, copy):
+            copy(result, acc[:])
+            nc.sync.dma_start(out_rows[:, :, j0 : j0 + acc.shape[2]], result)
 
-        nc.scalar.copy(
-            w2_bf[:].rearrange("p (a i) j -> p a j i", i=4), w2_raw[:].rearrange("p j (a i) -> p a j i", i=4)
-        )
-        nc.vector.tensor_scalar(u_early[:, 0, :], h[0][:, 0:EARLY], tap_of(0, 0), None, MULT)
-        nc.scalar.activation(u_early[:, 1, :], h[1][:, 0:EARLY], COPY, scale=tap_of(1, 0))
-        nc.vector.quantize_mx(
-            out=w2_codes[:].bitcast(FP8X4), scales=w2_scales[:], in_=w2_bf[:].rearrange("p c j -> p (c j)")
-        )
-        side = keep.tile([P, LATE_CHUNKS, PACK, LATE], F32, name="side", tag="w2_bf", align_bytes=64)
-        for d in range(1, D):
-            for t in (1, 0):
-                add_tap(u_early[:], 0, t, d)
-        for t in (2, 3):
-            nc.scalar.activation(u_early[:, t, :], h[t][:, 0:EARLY], COPY, scale=tap_of(t, 0))
-            late_products(t)
-        for t in (2, 3):
-            side_product(t, 0)
-        add_side(2, 0)
+        def cast_w2(b):
+            nc.scalar.copy(
+                w2_bf[b][:].rearrange("p (a i) j -> p a j i", i=4),
+                w2_raw[:, :, P * b : P * (b + 1)].rearrange("p j (a i) -> p a j i", i=4),
+            )
+
+        cast_w2(0)
+        for t in range(PACK):
+            first_tap(0, t)
+        cast_w2(1)
+        for b in range(N // P):
+            nc.vector.quantize_mx(
+                out=w2_codes[:, P * b : P * (b + 1)].bitcast(FP8X4),
+                scales=w2_scales[:, P * b : P * (b + 1)],
+                in_=w2_bf[b][:].rearrange("p c j -> p (c j)"),
+            )
+        for d in (2, 1, 0):
+            for t in (0, 1):
+                add_tap(0, t, d, d, HALF + d)
+        side = keep.tile([P, PACK, HALF], F32, name="side", align_bytes=64)
         for t in (0, 1):
-            late_products(t)
-            side_product(t, 1)
-        add_side(0, 1)
-        for d in range(1, D - 1):
+            first_tap(1, t)
+        for t in (0, 1):
+            side_product(t, 0)
+        add_side(0, 2, 0)
+        for t in (2, 3):
+            first_tap(1, t)
+            side_product(t, CHUNK)
+        add_side(0, PACK, CHUNK)
+        for d in (2, 1):
             for t in (2, 3):
-                add_tap(u_early[:], 0, t, d)
-        z_early = keep.tile([P, EARLY, PACK], BF16, name="z_early", align_bytes=64)
-        for j0 in range(0, EARLY, LATE):
+                add_tap(0, t, d, d, HALF + d)
+        z_early = keep.tile([P, HALF, PACK], BF16, name="z_early", align_bytes=64)
+        for j0 in range(0, HALF, CHUNK):
             for t in (2, 3):
-                add_tap(u_early[:, :, j0 : j0 + LATE], j0, t, D - 1)
-            silu_into(z_early[:, j0 : j0 + LATE, :], u_early[:, :, j0 : j0 + LATE])
-        acc_early = both_blocks(z_early, 0)
-        z_late = []
-        for c in range(LATE_CHUNKS):
-            for d in range(1, D - 1):
-                for t in (0, 1, 2, 3):
-                    add_tap(u_late[:, c], EARLY + LATE * c, t, d)
-            if c == 0:
-                for t in (0, 1):
-                    add_tap(u_late[:, c], EARLY, t, D - 1)
-            z_late.append(silu_z(u_late[:, c], EARLY + LATE * c, f"z_late{c}"))
-        j0 = EARLY + LATE
-        acc_mid = both_blocks(z_late[0], EARLY)
-        store_both(acc_early, 0, "early_result", nc.vector.tensor_copy)
-        codes, plane = quantized(z_late[1], j0)
-        store_both(acc_mid, EARLY, "shared", nc.scalar.copy)
+                add_tap(0, t, 0, j0, j0 + CHUNK)
+            silu_into(z_early[:, j0 : j0 + CHUNK, :], j0)
+        mid, last = HALF, HALF + CHUNK
+        for d in (2, 1):
+            for t in (2, 3, 0, 1):
+                add_tap(1, t, d, mid + d, last)
+        for t in (2, 3):
+            add_tap(1, t, 0, mid, last)
+        z_mid = keep.tile([P, CHUNK, PACK], BF16, name="z_mid", align_bytes=64)
+        silu_into(z_mid[:], mid)
+        acc_early = both_blocks(z_early, 0, "bank0_0")
+        for d in (2, 1):
+            for t in range(PACK):
+                add_tap(1, t, d, last, S)
+        z_last = keep.tile([P, CHUNK, PACK], BF16, name="z_last", align_bytes=64)
+        silu_into(z_last[:], last)
+        acc_mid = both_blocks(z_mid, mid, "bank0_1")
+        early_result = keep.tile([P, N // P, HALF], F32, name="early_result", align_bytes=64)
+        store_both(acc_early, 0, early_result[:], nc.vector.tensor_copy)
+        codes, plane = quantized(z_last, last)
+        store_both(acc_mid, mid, u[:, 0:2, last:S], nc.scalar.copy)
         for b, copy in ((0, nc.vector.tensor_copy), (1, nc.scalar.copy)):
-            acc = psum.tile([P, LATE], F32, name=f"acc_last{b}")
+            acc = psum.tile([P, CHUNK], F32, name=f"acc_last{b}", tag=f"bank0_{2 + b}")
             second_product(acc[:], b, codes, plane)
-            result = keep.tile([P, LATE], F32, name=f"result_last{b}", align_bytes=64)
+            result = keep.tile([P, CHUNK], F32, name=f"result_last{b}", align_bytes=64)
             copy(result[:], acc[:])
-            nc.sync.dma_start(out_rows[:, b, j0:S], result[:])
+            nc.sync.dma_start(out_rows[:, b, last:S], result[:])

@@ -25,29 +25,33 @@ PASSES = K // K_PASS
 QUADRANT = 32
 HALF = 256
 CHUNK = 128
-M_VECTOR_0 = 56
+M_VECTOR_0 = 84
 M_VECTOR_1 = 84
+W2_SCALAR = 64
 
 
 def tile_picked_dconv_silu_p_kernel(tc, x_words, x_scales, w1, w2, taps, offs, out):
     nc = tc.nc
     with ExitStack() as ctx:
         keep = ctx.enter_context(tc.tile_pool(name="keep", bufs=1))
+        placed = ctx.enter_context(tc.tile_pool(name="placed", bufs=1))
         psum = ctx.enter_context(tc.psum_pool(name="psum", bufs=1))
 
         offsets = keep.tile([P, S // 16], U16, name="offsets")
         words = [keep.tile([P, T], U16, name=f"words{g}", align_bytes=64) for g in range(PASSES)]
-        scales = keep.tile([P, PASSES, T], U8, name="scales", align_bytes=64)
+        scales = placed.tile([P, T], U8, name="scales", align_bytes=64, offset=T // 2)
+        moved_scales = keep.tile([P, S], U8, name="moved_scales", align_bytes=64)
+        picked_scales = keep.tile([P, S], U8, name="picked_scales", align_bytes=64)
         w1_raw = [keep.tile([P, PACK, H], F32, name=f"w1_raw{g}", align_bytes=64) for g in range(PASSES)]
-        w2_raw = keep.tile([P, PACK, N], F32, name="w2_raw", align_bytes=64)
         tap = keep.tile([P, PACK * D], F32, name="tap")
         zero_in = keep.tile([P, 1], F32, name="zero_in")
         zero_bias = keep.tile([P, 1], F32, name="zero_bias")
         u = keep.tile([P, PACK, S], F32, name="u", align_bytes=64)
 
-        nc.vector.memset(scales[:].rearrange("p g c -> p (g c)").bitcast(I32), 0)
+        nc.vector.memset(scales[:].bitcast(I32), 0)
         nc.vector.memset(zero_in[:], 0.0)
         nc.vector.memset(u[:, :, 0 : D - 1], 0.0)
+        nc.vector.memset(moved_scales[:].bitcast(I32), 0)
         nc.scalar.activation(zero_bias[:], zero_in[:], SILU)
 
         nc.sync.dma_start(words[0][:].bitcast(I32), x_words[0].bitcast(I32))
@@ -55,17 +59,15 @@ def tile_picked_dconv_silu_p_kernel(tc, x_words, x_scales, w1, w2, taps, offs, o
         nc.sync.dma_start(words[1][:].bitcast(I32), x_words[1].bitcast(I32))
         for r in range(4):
             nc.sync.dma_start(
-                scales[r:P:QUADRANT, :, :].bitcast(I32),
+                scales[r : P : QUADRANT // 2, :].bitcast(I32),
                 x_scales[:, r:16:4, :].rearrange("g q c -> q g c").bitcast(I32),
             )
         nc.sync.dma_start(w1_raw[0][:], w1[0:K_PASS, :].rearrange("(p j) c -> p j c", j=PACK))
         nc.sync.dma_start(w1_raw[1][:], w1[K_PASS:K, :].rearrange("(p j) c -> p j c", j=PACK))
         nc.sync.dma_start(tap[:], taps.rearrange("(p t) d -> p (t d)", t=PACK))
-        nc.sync.dma_start(w2_raw[:], w2.rearrange("(p j) c -> p j c", j=PACK))
 
         picked_words0 = keep.tile([P, S], U16, name="picked_words0", align_bytes=64)
-        picked_early1 = keep.tile([P, HALF], U16, name="picked_early1", tag="picked_early1", align_bytes=64)
-        picked_scales = [keep.tile([P, S], U8, name=f"picked_scales{g}", align_bytes=64) for g in range(PASSES)]
+        planes = [picked_scales, moved_scales]
         w1_bf = [
             [keep.tile([P, 2, P, PACK], BF16, name=f"w1_bf{g}_{a}", tag=f"w1_bf{g}_{a}", align_bytes=64) for a in range(2)]
             for g in range(PASSES)
@@ -93,15 +95,22 @@ def tile_picked_dconv_silu_p_kernel(tc, x_words, x_scales, w1, w2, taps, offs, o
                 lhsT=w1_codes[g][t][:].bitcast(FP8X4),
                 lhsT_scale=w1_scales[g][t][:],
                 rhs=moving.bitcast(FP4X4),
-                rhs_scale=picked_scales[g][:, HALF * half : HALF * (half + 1)],
+                rhs_scale=planes[g][:, HALF * half : HALF * (half + 1)],
                 start=opens,
                 stop=not opens,
             )
 
         nc.vector.tensor_copy(picked_words0[:], words[0][:].indirect(offsets[:]))
-        nc.vector.tensor_copy(picked_early1[:], words[1][:].indirect(offsets[:, 0 : HALF // 16]))
-        for g in range(PASSES):
-            nc.vector.tensor_copy(picked_scales[g][:], scales[:, g, :].indirect(offsets[:]))
+        nc.vector.tensor_copy(picked_scales[:], scales[:].indirect(offsets[:]))
+        for r in range(4):
+            nc.sync.dma_start(
+                moved_scales[r:P:QUADRANT, :].bitcast(I32),
+                picked_scales[QUADRANT // 2 + r : P : QUADRANT, :].bitcast(I32),
+            )
+        w2_raw = placed.tile([P, PACK, N], F32, name="w2_raw", align_bytes=64, offset=T)
+        nc.sync.dma_start(w2_raw[:], w2.rearrange("(p j) c -> p j c", j=PACK))
+        picked_words1 = placed.tile([P, S], U16, name="picked_words1", align_bytes=64, offset=0)
+        nc.vector.tensor_copy(picked_words1[:], words[1][:].indirect(offsets[:]))
         cast_w1(nc.scalar.copy, 0, 0, 0, P)
         cast_w1(nc.vector.tensor_copy, 0, 1, 0, M_VECTOR_0)
         cast_w1(nc.scalar.copy, 0, 1, M_VECTOR_0, P)
@@ -113,17 +122,12 @@ def tile_picked_dconv_silu_p_kernel(tc, x_words, x_scales, w1, w2, taps, offs, o
             cast_w1(nc.scalar.copy, 1, a, M_VECTOR_1, P)
         for t in range(PACK):
             quantize_w1(1, t)
-            first_product(1, t, 0, picked_early1[:], False)
-        picked_late1 = keep.tile([P, HALF], U16, name="picked_late1", tag="w1_bf1_0", align_bytes=64)
-        nc.vector.tensor_copy(picked_late1[:], words[1][:].indirect(offsets[:, HALF // 16 : S // 16]))
+            first_product(1, t, 0, picked_words1[:, 0:HALF], False)
         for t in range(PACK):
-            first_product(1, t, 1, picked_late1[:], True)
+            first_product(1, t, 1, picked_words1[:, HALF:S], True)
             first_product(0, t, 1, picked_words0[:, HALF:S], False)
 
-        w2_bf = [
-            keep.tile([P, P, PACK], BF16, name=f"w2_bf{b}", tag=tag, align_bytes=64)
-            for b, tag in enumerate(("w2_bf0", "picked_early1"))
-        ]
+        w2_bf = keep.tile([P, N, PACK], BF16, name="w2_bf", align_bytes=64)
         w2_codes = keep.tile([P, N], U32, name="w2_codes", align_bytes=64)
         w2_scales = keep.tile([P, N], U8, name="w2_scales", align_bytes=64)
         out_rows = out.rearrange("(b p) j -> p b j", p=P)
@@ -190,42 +194,42 @@ def tile_picked_dconv_silu_p_kernel(tc, x_words, x_scales, w1, w2, taps, offs, o
             copy(result, acc[:])
             nc.sync.dma_start(out_rows[:, :, j0 : j0 + acc.shape[2]], result)
 
-        def cast_w2(b):
-            nc.scalar.copy(
-                w2_bf[b][:].rearrange("p (a i) j -> p a j i", i=4),
-                w2_raw[:, :, P * b : P * (b + 1)].rearrange("p j (a i) -> p a j i", i=4),
+        def cast_w2(copy, c0, c1):
+            copy(
+                w2_bf[:, c0:c1, :].rearrange("p (a i) j -> p a j i", i=4),
+                w2_raw[:, :, c0:c1].rearrange("p j (a i) -> p a j i", i=4),
             )
 
-        cast_w2(0)
+        cast_w2(nc.scalar.copy, 0, W2_SCALAR)
+        cast_w2(nc.vector.tensor_copy, W2_SCALAR, N)
+        side_early = keep.tile([P, 2, HALF], F32, name="side_early", align_bytes=64)
         for t in range(PACK):
             first_tap(0, t)
-        cast_w2(1)
-        for b in range(N // P):
-            nc.vector.quantize_mx(
-                out=w2_codes[:, P * b : P * (b + 1)].bitcast(FP8X4),
-                scales=w2_scales[:, P * b : P * (b + 1)],
-                in_=w2_bf[b][:].rearrange("p c j -> p (c j)"),
-            )
+            if t >= 2:
+                nc.scalar.activation(side_early[:, t - 2, :], h[0][t][:], COPY, scale=tap_of(t, 0))
+                nc.gpsimd.tensor_tensor(u[:, t, 0:HALF], u[:, t, 0:HALF], side_early[:, t - 2, :], ADD)
         for d in (2, 1, 0):
             for t in (0, 1):
                 add_tap(0, t, d, d, HALF + d)
+            if d == 2:
+                nc.vector.quantize_mx(
+                    out=w2_codes[:].bitcast(FP8X4), scales=w2_scales[:], in_=w2_bf[:].rearrange("p c j -> p (c j)")
+                )
         side = keep.tile([P, PACK, HALF], F32, name="side", align_bytes=64)
         for t in (0, 1):
             first_tap(1, t)
-        for t in (0, 1):
             side_product(t, 0)
         add_side(0, 2, 0)
         for t in (2, 3):
             first_tap(1, t)
             side_product(t, CHUNK)
         add_side(0, PACK, CHUNK)
-        for d in (2, 1):
-            for t in (2, 3):
-                add_tap(0, t, d, d, HALF + d)
+        for t in (2, 3):
+            add_tap(0, t, 2, 2, HALF + 2)
         z_early = keep.tile([P, HALF, PACK], BF16, name="z_early", align_bytes=64)
         for j0 in range(0, HALF, CHUNK):
             for t in (2, 3):
-                add_tap(0, t, 0, j0, j0 + CHUNK)
+                add_tap(0, t, 1, max(j0, 1), j0 + CHUNK + j0 // CHUNK)
             silu_into(z_early[:, j0 : j0 + CHUNK, :], j0)
         mid, last = HALF, HALF + CHUNK
         for d in (2, 1):

@@ -25,8 +25,9 @@ PASSES = K // K_PASS
 QUADRANT = 32
 HALF = 256
 CHUNK = 128
+END = 64
 M_VECTOR_0 = 84
-M_VECTOR_1 = 84
+M_VECTOR_1 = (84, 64)
 W2_SCALAR = 64
 
 
@@ -118,8 +119,8 @@ def tile_picked_dconv_silu_p_kernel(tc, x_words, x_scales, w1, w2, taps, offs, o
             quantize_w1(0, t)
             first_product(0, t, 0, picked_words0[:, 0:HALF], True)
         for a in range(2):
-            cast_w1(nc.vector.tensor_copy, 1, a, 0, M_VECTOR_1)
-            cast_w1(nc.scalar.copy, 1, a, M_VECTOR_1, P)
+            cast_w1(nc.vector.tensor_copy, 1, a, 0, M_VECTOR_1[a])
+            cast_w1(nc.scalar.copy, 1, a, M_VECTOR_1[a], P)
         for t in range(PACK):
             quantize_w1(1, t)
             first_product(1, t, 0, picked_words1[:, 0:HALF], False)
@@ -161,7 +162,7 @@ def tile_picked_dconv_silu_p_kernel(tc, x_words, x_scales, w1, w2, taps, offs, o
         def silu_into(z, j0):
             nc.scalar.activation(
                 z.rearrange("p (a i) t -> p a t i", i=4),
-                u[:, :, j0 : j0 + CHUNK].rearrange("p t (a i) -> p a t i", i=4),
+                u[:, :, j0 : j0 + z.shape[1]].rearrange("p t (a i) -> p a t i", i=4),
                 SILU,
                 bias=zero_bias[:],
             )
@@ -231,28 +232,36 @@ def tile_picked_dconv_silu_p_kernel(tc, x_words, x_scales, w1, w2, taps, offs, o
             for t in (2, 3):
                 add_tap(0, t, 1, max(j0, 1), j0 + CHUNK + j0 // CHUNK)
             silu_into(z_early[:, j0 : j0 + CHUNK, :], j0)
-        mid, last = HALF, HALF + CHUNK
+        mid, last, end = HALF, HALF + CHUNK, S - END
         for d in (2, 1):
             for t in (2, 3, 0, 1):
                 add_tap(1, t, d, mid + d, last)
+        codes, plane = quantized(z_early, 0)
+        acc_early = [psum.tile([P, HALF], F32, name=f"acc_early{b}", tag=f"bank0_{b}") for b in range(N // P)]
+        for b in range(N // P):
+            second_product(acc_early[b][:], b, codes, plane)
         for t in (2, 3):
             add_tap(1, t, 0, mid, last)
         z_mid = keep.tile([P, CHUNK, PACK], BF16, name="z_mid", align_bytes=64)
         silu_into(z_mid[:], mid)
-        acc_early = both_blocks(z_early, 0, "bank0_0")
-        for d in (2, 1):
+        for t in range(PACK):
+            add_tap(1, t, 2, last, S)
+        z_small = []
+        for j0 in (last, end):
             for t in range(PACK):
-                add_tap(1, t, d, last, S)
-        z_last = keep.tile([P, CHUNK, PACK], BF16, name="z_last", align_bytes=64)
-        silu_into(z_last[:], last)
-        acc_mid = both_blocks(z_mid, mid, "bank0_1")
-        early_result = keep.tile([P, N // P, HALF], F32, name="early_result", align_bytes=64)
-        store_both(acc_early, 0, early_result[:], nc.vector.tensor_copy)
-        codes, plane = quantized(z_last, last)
-        store_both(acc_mid, mid, u[:, 0:2, last:S], nc.scalar.copy)
-        for b, copy in ((0, nc.vector.tensor_copy), (1, nc.scalar.copy)):
-            acc = psum.tile([P, CHUNK], F32, name=f"acc_last{b}", tag=f"bank0_{2 + b}")
-            second_product(acc[:], b, codes, plane)
-            result = keep.tile([P, CHUNK], F32, name=f"result_last{b}", align_bytes=64)
-            copy(result[:], acc[:])
-            nc.sync.dma_start(out_rows[:, b, last:S], result[:])
+                add_tap(1, t, 1, j0, j0 + END)
+            z_small.append(keep.tile([P, END, PACK], BF16, name=f"z{j0}", tag=f"z{j0}", align_bytes=64))
+            silu_into(z_small[-1][:], j0)
+        acc_mid = both_blocks(z_mid, mid, "bank0_2")
+        early_result = keep.tile([P, HALF], F32, name="early_result", align_bytes=64)
+        nc.vector.tensor_copy(early_result[:], acc_early[0][:])
+        nc.sync.dma_start(out_rows[:, 0, 0:HALF], early_result[:])
+        acc_last = both_blocks(z_small[0], last, "bank0_3")
+        nc.scalar.copy(u[:, 0, HALF:S], acc_early[1][:])
+        nc.sync.dma_start(out_rows[:, 1, 0:HALF], u[:, 0, HALF:S])
+        acc_end = both_blocks(z_small[1], end, "bank1_0")
+        store_both(acc_mid, mid, u[:, 1:3, last:S], nc.scalar.copy)
+        last_result = keep.tile([P, N // P, END], F32, name="last_result", tag=f"z{end}", align_bytes=64)
+        store_both(acc_last, last, last_result[:], nc.vector.tensor_copy)
+        end_result = keep.tile([P, N // P, END], F32, name="end_result", align_bytes=64)
+        store_both(acc_end, end, end_result[:], nc.vector.tensor_copy)

@@ -228,9 +228,9 @@ def tile_picked_dconv_silu_p_kernel(tc, x_words, x_scales, w1, w2, taps, offs, o
         for t in (2, 3):
             add_tap(0, t, 2, 2, HALF + 2)
         z_early = keep.tile([P, HALF, PACK], BF16, name="z_early", align_bytes=64)
+        add_tap(0, 2, 1, 1, HALF + 1)
         for j0 in range(0, HALF, CHUNK):
-            for t in (2, 3):
-                add_tap(0, t, 1, max(j0, 1), j0 + CHUNK + j0 // CHUNK)
+            add_tap(0, 3, 1, max(j0, 1), j0 + CHUNK + j0 // CHUNK)
             silu_into(z_early[:, j0 : j0 + CHUNK, :], j0)
         mid, last, end = HALF, HALF + CHUNK, S - END
         for d in (2, 1):

@@ -28,7 +28,6 @@ CHUNK = 128
 END = 64
 M_VECTOR_0 = 84
 M_VECTOR_1 = (84, 64)
-W2_SCALAR = 64
 
 
 def tile_picked_dconv_silu_p_kernel(tc, x_words, x_scales, w1, w2, taps, offs, out):
@@ -146,7 +145,7 @@ def tile_picked_dconv_silu_p_kernel(tc, x_words, x_scales, w1, w2, taps, offs, o
             nc.vector.scalar_tensor_tensor(
                 out=u[:, t, j0:j1],
                 in0=h[half][t][:, j0 - base : j1 - base],
-                scalar=tap_of(t, d),
+                scalar=vector_tap[:, D * t + d : D * t + d + 1],
                 in1=u[:, t, j0:j1],
                 op0=MULT,
                 op1=ADD,
@@ -201,21 +200,27 @@ def tile_picked_dconv_silu_p_kernel(tc, x_words, x_scales, w1, w2, taps, offs, o
                 w2_raw[:, :, c0:c1].rearrange("p j (a i) -> p a j i", i=4),
             )
 
-        cast_w2(nc.scalar.copy, 0, W2_SCALAR)
-        cast_w2(nc.vector.tensor_copy, W2_SCALAR, N)
+        cast_w2(nc.vector.tensor_copy, 0, N)
+        vector_tap = placed.tile([P, PACK * D], F32, name="vector_tap", align_bytes=64, offset=T)
+        nc.vector.tensor_copy(vector_tap[:], tap[:])
+        nc.vector.quantize_mx(
+            out=w2_codes[:].bitcast(FP8X4), scales=w2_scales[:], in_=w2_bf[:].rearrange("p c j -> p (c j)")
+        )
         side_early = keep.tile([P, 2, HALF], F32, name="side_early", align_bytes=64)
         for t in range(PACK):
             first_tap(0, t)
             if t >= 2:
                 nc.scalar.activation(side_early[:, t - 2, :], h[0][t][:], COPY, scale=tap_of(t, 0))
                 nc.gpsimd.tensor_tensor(u[:, t, 0:HALF], u[:, t, 0:HALF], side_early[:, t - 2, :], ADD)
-        for d in (2, 1, 0):
+        for d in (2, 1):
             for t in (0, 1):
-                add_tap(0, t, d, d, HALF + d)
-            if d == 2:
-                nc.vector.quantize_mx(
-                    out=w2_codes[:].bitcast(FP8X4), scales=w2_scales[:], in_=w2_bf[:].rearrange("p c j -> p (c j)")
-                )
+                for c0 in (0, CHUNK):
+                    add_tap(0, t, d, c0 + d, c0 + CHUNK + d)
+        for t, d in ((2, 2), (0, 0), (1, 0)):
+            add_tap(0, t, d, d, HALF + d)
+        for c0 in (0, CHUNK):
+            add_tap(0, 3, 2, c0 + 2, c0 + CHUNK + 2)
+        add_tap(0, 2, 1, 1, HALF + 1)
         side = keep.tile([P, PACK, HALF], F32, name="side", align_bytes=64)
         for t in (0, 1):
             first_tap(1, t)
@@ -225,10 +230,7 @@ def tile_picked_dconv_silu_p_kernel(tc, x_words, x_scales, w1, w2, taps, offs, o
             first_tap(1, t)
             side_product(t, CHUNK)
         add_side(0, PACK, CHUNK)
-        for t in (2, 3):
-            add_tap(0, t, 2, 2, HALF + 2)
         z_early = keep.tile([P, HALF, PACK], BF16, name="z_early", align_bytes=64)
-        add_tap(0, 2, 1, 1, HALF + 1)
         for j0 in range(0, HALF, CHUNK):
             add_tap(0, 3, 1, max(j0, 1), j0 + CHUNK + j0 // CHUNK)
             silu_into(z_early[:, j0 : j0 + CHUNK, :], j0)
@@ -236,16 +238,16 @@ def tile_picked_dconv_silu_p_kernel(tc, x_words, x_scales, w1, w2, taps, offs, o
         for d in (2, 1):
             for t in (2, 3, 0, 1):
                 add_tap(1, t, d, mid + d, last)
-        codes, plane = quantized(z_early, 0)
-        acc_early = [psum.tile([P, HALF], F32, name=f"acc_early{b}", tag=f"bank0_{b}") for b in range(N // P)]
-        for b in range(N // P):
-            second_product(acc_early[b][:], b, codes, plane)
         for t in (2, 3):
             add_tap(1, t, 0, mid, last)
         z_mid = keep.tile([P, CHUNK, PACK], BF16, name="z_mid", align_bytes=64)
         silu_into(z_mid[:], mid)
         for t in range(PACK):
             add_tap(1, t, 2, last, S)
+        codes, plane = quantized(z_early, 0)
+        acc_early = [psum.tile([P, HALF], F32, name=f"acc_early{b}", tag=f"bank0_{b}") for b in range(N // P)]
+        for b in range(N // P):
+            second_product(acc_early[b][:], b, codes, plane)
         z_small = []
         for j0 in (last, end):
             for t in range(PACK):

@@ -263,7 +263,7 @@ def tile_picked_dconv_silu_p_kernel(tc, x_words, x_scales, w1, w2, taps, offs, o
         nc.sync.dma_start(out_rows[:, 1, 0:HALF], u[:, 0, HALF:S])
         acc_end = both_blocks(z_small[1], end, "bank1_0")
         store_both(acc_mid, mid, u[:, 1:3, last:S], nc.scalar.copy)
-        last_result = keep.tile([P, N // P, END], F32, name="last_result", tag=f"z{end}", align_bytes=64)
-        store_both(acc_last, last, last_result[:], nc.vector.tensor_copy)
-        end_result = keep.tile([P, N // P, END], F32, name="end_result", align_bytes=64)
-        store_both(acc_end, end, end_result[:], nc.vector.tensor_copy)
+        last_result = keep.tile([P, N // P, CHUNK], F32, name="last_result", tag=f"z{end}", align_bytes=64)
+        nc.vector.tensor_copy(last_result[:, :, 0:END], acc_last[:])
+        nc.vector.tensor_copy(last_result[:, :, END:CHUNK], acc_end[:])
+        nc.sync.dma_start(out_rows[:, :, last:S], last_result[:])

@@ -200,12 +200,16 @@ def tile_picked_dconv_silu_p_kernel(tc, x_words, x_scales, w1, w2, taps, offs, o
                 w2_raw[:, :, c0:c1].rearrange("p j (a i) -> p a j i", i=4),
             )
 
-        cast_w2(nc.vector.tensor_copy, 0, N)
-        vector_tap = placed.tile([P, PACK * D], F32, name="vector_tap", align_bytes=64, offset=T)
-        nc.vector.tensor_copy(vector_tap[:], tap[:])
-        nc.vector.quantize_mx(
-            out=w2_codes[:].bitcast(FP8X4), scales=w2_scales[:], in_=w2_bf[:].rearrange("p c j -> p (c j)")
-        )
+        for b in range(N // P):
+            cast_w2(nc.vector.tensor_copy, P * b, P * (b + 1))
+        vector_tap = w2_raw[:, 0, 0 : PACK * D]
+        nc.vector.tensor_copy(vector_tap, tap[:])
+        for b in range(N // P):
+            nc.vector.quantize_mx(
+                out=w2_codes[:, P * b : P * (b + 1)].bitcast(FP8X4),
+                scales=w2_scales[:, P * b : P * (b + 1)],
+                in_=w2_bf[:, P * b : P * (b + 1), :].rearrange("p c j -> p (c j)"),
+            )
         side_early = keep.tile([P, 2, HALF], F32, name="side_early", align_bytes=64)
         for t in range(PACK):
             first_tap(0, t)
@@ -216,7 +220,7 @@ def tile_picked_dconv_silu_p_kernel(tc, x_words, x_scales, w1, w2, taps, offs, o
             for t in (0, 1):
                 for c0 in (0, CHUNK):
                     add_tap(0, t, d, c0 + d, c0 + CHUNK + d)
-        for t, d in ((2, 2), (0, 0), (1, 0)):
+        for t, d in ((0, 0), (2, 2), (1, 0)):
             add_tap(0, t, d, d, HALF + d)
         for c0 in (0, CHUNK):
             add_tap(0, 3, 2, c0 + 2, c0 + CHUNK + 2)
@@ -261,9 +265,13 @@ def tile_picked_dconv_silu_p_kernel(tc, x_words, x_scales, w1, w2, taps, offs, o
         acc_last = both_blocks(z_small[0], last, "bank0_3")
         nc.scalar.copy(u[:, 0, HALF:S], acc_early[1][:])
         nc.sync.dma_start(out_rows[:, 1, 0:HALF], u[:, 0, HALF:S])
-        acc_end = both_blocks(z_small[1], end, "bank1_0")
+        codes, plane = quantized(z_small[1], end)
+        acc_end = [psum.tile([P, END], F32, name=f"acc_end{b}", tag=f"bank1_{b}") for b in range(N // P)]
+        for b in range(N // P):
+            second_product(acc_end[b][:], b, codes, plane)
         store_both(acc_mid, mid, u[:, 1:3, last:S], nc.scalar.copy)
         last_result = keep.tile([P, N // P, CHUNK], F32, name="last_result", tag=f"z{end}", align_bytes=64)
         nc.vector.tensor_copy(last_result[:, :, 0:END], acc_last[:])
-        nc.vector.tensor_copy(last_result[:, :, END:CHUNK], acc_end[:])
-        nc.sync.dma_start(out_rows[:, :, last:S], last_result[:])
+        for b in range(N // P):
+            nc.vector.tensor_copy(last_result[:, b, END:CHUNK], acc_end[b][:])
+            nc.sync.dma_start(out_rows[:, b, last:S], last_result[:, b, :])

@@ -244,7 +244,7 @@ def tile_picked_dconv_silu_p_kernel(tc, x_words, x_scales, w1, w2, taps, offs, o
                 add_tap(1, t, d, mid + d, last)
         for t in (2, 3):
             add_tap(1, t, 0, mid, last)
-        z_mid = keep.tile([P, CHUNK, PACK], BF16, name="z_mid", align_bytes=64)
+        z_mid = keep.tile([P, CHUNK, PACK], BF16, name="z_mid", tag="z_mid", align_bytes=64)
         silu_into(z_mid[:], mid)
         for t in range(PACK):
             add_tap(1, t, 2, last, S)
@@ -263,8 +263,9 @@ def tile_picked_dconv_silu_p_kernel(tc, x_words, x_scales, w1, w2, taps, offs, o
         nc.vector.tensor_copy(early_result[:], acc_early[0][:])
         nc.sync.dma_start(out_rows[:, 0, 0:HALF], early_result[:])
         acc_last = both_blocks(z_small[0], last, "bank0_3")
-        nc.scalar.copy(u[:, 0, HALF:S], acc_early[1][:])
-        nc.sync.dma_start(out_rows[:, 1, 0:HALF], u[:, 0, HALF:S])
+        second_result = keep.tile([P, HALF], F32, name="second_result", tag="z_mid", align_bytes=64)
+        nc.scalar.copy(second_result[:], acc_early[1][:])
+        nc.sync.dma_start(out_rows[:, 1, 0:HALF], second_result[:])
         codes, plane = quantized(z_small[1], end)
         acc_end = [psum.tile([P, END], F32, name=f"acc_end{b}", tag=f"bank1_{b}") for b in range(N // P)]
         for b in range(N // P):

@@ -38,15 +38,15 @@ def tile_picked_dconv_silu_p_kernel(tc, x_words, x_scales, w1, w2, taps, offs, o
         psum = ctx.enter_context(tc.psum_pool(name="psum", bufs=1))
 
         offsets = keep.tile([P, S // 16], U16, name="offsets")
-        words = [keep.tile([P, T], U16, name=f"words{g}", align_bytes=64) for g in range(PASSES)]
-        scales = placed.tile([P, T], U8, name="scales", align_bytes=64, offset=T // 2)
-        moved_scales = keep.tile([P, S], U8, name="moved_scales", align_bytes=64)
-        picked_scales = keep.tile([P, S], U8, name="picked_scales", align_bytes=64)
-        w1_raw = [keep.tile([P, PACK, H], F32, name=f"w1_raw{g}", align_bytes=64) for g in range(PASSES)]
+        words = [keep.tile([P, T], U16, name=f"words{g}", align_bytes=256) for g in range(PASSES)]
+        scales = placed.tile([P, T], U8, name="scales", align_bytes=256, offset=T // 2)
+        moved_scales = keep.tile([P, S], U8, name="moved_scales", align_bytes=256)
+        picked_scales = keep.tile([P, S], U8, name="picked_scales", align_bytes=256)
+        w1_raw = [keep.tile([P, PACK, H], F32, name=f"w1_raw{g}", align_bytes=256) for g in range(PASSES)]
         tap = keep.tile([P, PACK * D], F32, name="tap")
         zero_in = keep.tile([P, 1], F32, name="zero_in")
         zero_bias = keep.tile([P, 1], F32, name="zero_bias")
-        u = keep.tile([P, PACK, S], F32, name="u", align_bytes=64)
+        u = keep.tile([P, PACK, S], F32, name="u", align_bytes=256)
 
         nc.vector.memset(scales[:].bitcast(I32), 0)
         nc.vector.memset(zero_in[:], 0.0)
@@ -66,14 +66,14 @@ def tile_picked_dconv_silu_p_kernel(tc, x_words, x_scales, w1, w2, taps, offs, o
         nc.sync.dma_start(w1_raw[1][:], w1[K_PASS:K, :].rearrange("(p j) c -> p j c", j=PACK))
         nc.sync.dma_start(tap[:], taps.rearrange("(p t) d -> p (t d)", t=PACK))
 
-        picked_words0 = keep.tile([P, S], U16, name="picked_words0", align_bytes=64)
+        picked_words0 = keep.tile([P, S], U16, name="picked_words0", align_bytes=256)
         planes = [picked_scales, moved_scales]
         w1_bf = [
-            [keep.tile([P, 2, P, PACK], BF16, name=f"w1_bf{g}_{a}", tag=f"w1_bf{g}_{a}", align_bytes=64) for a in range(2)]
+            [keep.tile([P, 2, P, PACK], BF16, name=f"w1_bf{g}_{a}", tag=f"w1_bf{g}_{a}", align_bytes=256) for a in range(2)]
             for g in range(PASSES)
         ]
-        w1_codes = [[keep.tile([P, P], U32, name=f"w1_codes{g}_{t}", align_bytes=64) for t in range(PACK)] for g in range(PASSES)]
-        w1_scales = [[keep.tile([P, P], U8, name=f"w1_scales{g}_{t}", align_bytes=64) for t in range(PACK)] for g in range(PASSES)]
+        w1_codes = [[keep.tile([P, P], U32, name=f"w1_codes{g}_{t}", align_bytes=256) for t in range(PACK)] for g in range(PASSES)]
+        w1_scales = [[keep.tile([P, P], U8, name=f"w1_scales{g}_{t}", align_bytes=256) for t in range(PACK)] for g in range(PASSES)]
         h = [[psum.tile([P, HALF], F32, name=f"h{half}_{t}", tag=f"bank{half}_{t}") for t in range(PACK)] for half in range(2)]
 
         def cast_w1(copy, g, a, m0, m1):
@@ -107,9 +107,9 @@ def tile_picked_dconv_silu_p_kernel(tc, x_words, x_scales, w1, w2, taps, offs, o
                 moved_scales[r:P:QUADRANT, :].bitcast(I32),
                 picked_scales[QUADRANT // 2 + r : P : QUADRANT, :].bitcast(I32),
             )
-        w2_raw = placed.tile([P, PACK, N], F32, name="w2_raw", align_bytes=64, offset=T)
+        w2_raw = placed.tile([P, PACK, N], F32, name="w2_raw", align_bytes=256, offset=T)
         nc.sync.dma_start(w2_raw[:], w2.rearrange("(p j) c -> p j c", j=PACK))
-        picked_words1 = placed.tile([P, S], U16, name="picked_words1", align_bytes=64, offset=0)
+        picked_words1 = placed.tile([P, S], U16, name="picked_words1", align_bytes=256, offset=0)
         nc.vector.tensor_copy(picked_words1[:], words[1][:].indirect(offsets[:]))
         cast_w1(nc.scalar.copy, 0, 0, 0, P)
         cast_w1(nc.vector.tensor_copy, 0, 1, 0, M_VECTOR_0)
@@ -127,9 +127,9 @@ def tile_picked_dconv_silu_p_kernel(tc, x_words, x_scales, w1, w2, taps, offs, o
             first_product(1, t, 1, picked_words1[:, HALF:S], True)
             first_product(0, t, 1, picked_words0[:, HALF:S], False)
 
-        w2_bf = keep.tile([P, N, PACK], BF16, name="w2_bf", align_bytes=64)
-        w2_codes = keep.tile([P, N], U32, name="w2_codes", align_bytes=64)
-        w2_scales = keep.tile([P, N], U8, name="w2_scales", align_bytes=64)
+        w2_bf = keep.tile([P, N, PACK], BF16, name="w2_bf", align_bytes=256)
+        w2_codes = keep.tile([P, N], U32, name="w2_codes", align_bytes=256)
+        w2_scales = keep.tile([P, N], U8, name="w2_scales", align_bytes=256)
         out_rows = out.rearrange("(b p) j -> p b j", p=P)
 
         def tap_of(t, d):
@@ -167,8 +167,8 @@ def tile_picked_dconv_silu_p_kernel(tc, x_words, x_scales, w1, w2, taps, offs, o
             )
 
         def quantized(z, j0):
-            codes = keep.tile([P, z.shape[1]], U32, name=f"z_codes{j0}", align_bytes=64)
-            plane = keep.tile([P, z.shape[1]], U8, name=f"z_scales{j0}", align_bytes=64)
+            codes = keep.tile([P, z.shape[1]], U32, name=f"z_codes{j0}", align_bytes=256)
+            plane = keep.tile([P, z.shape[1]], U8, name=f"z_scales{j0}", align_bytes=256)
             nc.vector.quantize_mx(out=codes[:].bitcast(FP8X4), scales=plane[:], in_=z[:].rearrange("p j t -> p (j t)"))
             return codes, plane
 
@@ -210,7 +210,7 @@ def tile_picked_dconv_silu_p_kernel(tc, x_words, x_scales, w1, w2, taps, offs, o
                 scales=w2_scales[:, P * b : P * (b + 1)],
                 in_=w2_bf[:, P * b : P * (b + 1), :].rearrange("p c j -> p (c j)"),
             )
-        side_early = keep.tile([P, 2, HALF], F32, name="side_early", align_bytes=64)
+        side_early = keep.tile([P, 2, HALF], F32, name="side_early", align_bytes=256)
         for t in range(PACK):
             first_tap(0, t)
             if t >= 2:
@@ -225,7 +225,7 @@ def tile_picked_dconv_silu_p_kernel(tc, x_words, x_scales, w1, w2, taps, offs, o
         for c0 in (0, CHUNK):
             add_tap(0, 3, 2, c0 + 2, c0 + CHUNK + 2)
         add_tap(0, 2, 1, 1, HALF + 1)
-        side = keep.tile([P, PACK, HALF], F32, name="side", align_bytes=64)
+        side = keep.tile([P, PACK, HALF], F32, name="side", align_bytes=256)
         for t in (0, 1):
             first_tap(1, t)
             side_product(t, 0)
@@ -234,7 +234,7 @@ def tile_picked_dconv_silu_p_kernel(tc, x_words, x_scales, w1, w2, taps, offs, o
             first_tap(1, t)
             side_product(t, CHUNK)
         add_side(0, PACK, CHUNK)
-        z_early = keep.tile([P, HALF, PACK], BF16, name="z_early", align_bytes=64)
+        z_early = keep.tile([P, HALF, PACK], BF16, name="z_early", align_bytes=256)
         for j0 in range(0, HALF, CHUNK):
             add_tap(0, 3, 1, max(j0, 1), j0 + CHUNK + j0 // CHUNK)
             silu_into(z_early[:, j0 : j0 + CHUNK, :], j0)
@@ -244,7 +244,7 @@ def tile_picked_dconv_silu_p_kernel(tc, x_words, x_scales, w1, w2, taps, offs, o
                 add_tap(1, t, d, mid + d, last)
         for t in (2, 3):
             add_tap(1, t, 0, mid, last)
-        z_mid = keep.tile([P, CHUNK, PACK], BF16, name="z_mid", tag="z_mid", align_bytes=64)
+        z_mid = keep.tile([P, CHUNK, PACK], BF16, name="z_mid", tag="z_mid", align_bytes=256)
         silu_into(z_mid[:], mid)
         for t in range(PACK):
             add_tap(1, t, 2, last, S)
@@ -256,14 +256,14 @@ def tile_picked_dconv_silu_p_kernel(tc, x_words, x_scales, w1, w2, taps, offs, o
         for j0 in (last, end):
             for t in range(PACK):
                 add_tap(1, t, 1, j0, j0 + END)
-            z_small.append(keep.tile([P, END, PACK], BF16, name=f"z{j0}", tag=f"z{j0}", align_bytes=64))
+            z_small.append(keep.tile([P, END, PACK], BF16, name=f"z{j0}", tag=f"z{j0}", align_bytes=256))
             silu_into(z_small[-1][:], j0)
         acc_mid = both_blocks(z_mid, mid, "bank0_2")
-        early_result = keep.tile([P, HALF], F32, name="early_result", align_bytes=64)
+        early_result = keep.tile([P, HALF], F32, name="early_result", align_bytes=256)
         nc.vector.tensor_copy(early_result[:], acc_early[0][:])
         nc.sync.dma_start(out_rows[:, 0, 0:HALF], early_result[:])
         acc_last = both_blocks(z_small[0], last, "bank0_3")
-        second_result = keep.tile([P, HALF], F32, name="second_result", tag="z_mid", align_bytes=64)
+        second_result = keep.tile([P, HALF], F32, name="second_result", tag="z_mid", align_bytes=256)
         nc.scalar.copy(second_result[:], acc_early[1][:])
         nc.sync.dma_start(out_rows[:, 1, 0:HALF], second_result[:])
         codes, plane = quantized(z_small[1], end)
@@ -271,7 +271,7 @@ def tile_picked_dconv_silu_p_kernel(tc, x_words, x_scales, w1, w2, taps, offs, o
         for b in range(N // P):
             second_product(acc_end[b][:], b, codes, plane)
         store_both(acc_mid, mid, u[:, 1:3, last:S], nc.scalar.copy)
-        last_result = keep.tile([P, N // P, CHUNK], F32, name="last_result", tag=f"z{end}", align_bytes=64)
+        last_result = keep.tile([P, N // P, CHUNK], F32, name="last_result", tag=f"z{end}", align_bytes=256)
         nc.vector.tensor_copy(last_result[:, :, 0:END], acc_last[:])
         for b in range(N // P):
             nc.vector.tensor_copy(last_result[:, b, END:CHUNK], acc_end[b][:])

from contextlib import ExitStack

import concourse.mybir as mybir

K, T, S, D, H, N = 1024, 1024, 512, 4, 512, 256
FLOPS = 2 * K * H * S + 2 * H * N * S

F32 = mybir.dt.float32
BF16 = mybir.dt.bfloat16
I32 = mybir.dt.int32
U32 = mybir.dt.uint32
U16 = mybir.dt.uint16
U8 = mybir.dt.uint8
FP8X4 = mybir.dt.float8_e4m3fn_x4
FP4X4 = mybir.dt.float4_e2m1fn_x4
MULT = mybir.AluOpType.mult
ADD = mybir.AluOpType.add
COPY = mybir.ActivationFunctionType.Copy
SILU = mybir.ActivationFunctionType.Silu

P = 128
PACK = 4
K_PASS = P * PACK
PASSES = K // K_PASS
QUADRANT = 32
HALF = 256
CHUNK = 128
END = 64
M_VECTOR_0 = 84
M_VECTOR_1 = (84, 64)


def tile_picked_dconv_silu_p_kernel(tc, x_words, x_scales, w1, w2, taps, offs, out):
    nc = tc.nc
    with ExitStack() as ctx:
        keep = ctx.enter_context(tc.tile_pool(name="keep", bufs=1))
        placed = ctx.enter_context(tc.tile_pool(name="placed", bufs=1))
        psum = ctx.enter_context(tc.psum_pool(name="psum", bufs=1))

        offsets = keep.tile([P, S // 16], U16, name="offsets")
        words = [keep.tile([P, T], U16, name=f"words{g}", align_bytes=256) for g in range(PASSES)]
        scales = placed.tile([P, T], U8, name="scales", align_bytes=256, offset=T // 2)
        moved_scales = keep.tile([P, S], U8, name="moved_scales", align_bytes=256)
        picked_scales = keep.tile([P, S], U8, name="picked_scales", align_bytes=256)
        w1_raw = [keep.tile([P, PACK, H], F32, name=f"w1_raw{g}", align_bytes=256) for g in range(PASSES)]
        tap = keep.tile([P, PACK * D], F32, name="tap")
        zero_in = keep.tile([P, 1], F32, name="zero_in")
        zero_bias = keep.tile([P, 1], F32, name="zero_bias")
        u = keep.tile([P, PACK, S], F32, name="u", align_bytes=256)

        nc.vector.memset(scales[:].bitcast(I32), 0)
        nc.vector.memset(zero_in[:], 0.0)
        nc.vector.memset(u[:, :, 0 : D - 1], 0.0)
        nc.vector.memset(moved_scales[:].bitcast(I32), 0)
        nc.scalar.activation(zero_bias[:], zero_in[:], SILU)

        nc.sync.dma_start(words[0][:].bitcast(I32), x_words[0].bitcast(I32))
        nc.sync.dma_start(offsets[:], offs)
        nc.sync.dma_start(words[1][:].bitcast(I32), x_words[1].bitcast(I32))
        for r in range(4):
            nc.sync.dma_start(
                scales[r : P : QUADRANT // 2, :].bitcast(I32),
                x_scales[:, r:16:4, :].rearrange("g q c -> q g c").bitcast(I32),
            )
        nc.sync.dma_start(w1_raw[0][:], w1[0:K_PASS, :].rearrange("(p j) c -> p j c", j=PACK))
        nc.sync.dma_start(w1_raw[1][:], w1[K_PASS:K, :].rearrange("(p j) c -> p j c", j=PACK))
        nc.sync.dma_start(tap[:], taps.rearrange("(p t) d -> p (t d)", t=PACK))

        picked_words0 = keep.tile([P, S], U16, name="picked_words0", align_bytes=256)
        planes = [picked_scales, moved_scales]
        w1_bf = [
            [keep.tile([P, 2, P, PACK], BF16, name=f"w1_bf{g}_{a}", tag=f"w1_bf{g}_{a}", align_bytes=256) for a in range(2)]
            for g in range(PASSES)
        ]
        w1_codes = [[keep.tile([P, P], U32, name=f"w1_codes{g}_{t}", align_bytes=256) for t in range(PACK)] for g in range(PASSES)]
        w1_scales = [[keep.tile([P, P], U8, name=f"w1_scales{g}_{t}", align_bytes=256) for t in range(PACK)] for g in range(PASSES)]
        h = [[psum.tile([P, HALF], F32, name=f"h{half}_{t}", tag=f"bank{half}_{t}") for t in range(PACK)] for half in range(2)]

        def cast_w1(copy, g, a, m0, m1):
            copy(
                w1_bf[g][a][:, :, m0:m1, :].rearrange("p t m j -> p m j t"),
                w1_raw[g][:].rearrange("p j (m t) -> p m j t", t=PACK)[:, m0:m1, :, 2 * a : 2 * a + 2],
            )

        def quantize_w1(g, t):
            nc.vector.quantize_mx(
                out=w1_codes[g][t][:].bitcast(FP8X4),
                scales=w1_scales[g][t][:],
                in_=w1_bf[g][t // 2][:, t % 2, :, :].rearrange("p m j -> p (m j)"),
            )

        def first_product(g, t, half, moving, opens):
            nc.tensor.matmul_mx(
                out=h[half][t][:],
                lhsT=w1_codes[g][t][:].bitcast(FP8X4),
                lhsT_scale=w1_scales[g][t][:],
                rhs=moving.bitcast(FP4X4),
                rhs_scale=planes[g][:, HALF * half : HALF * (half + 1)],
                start=opens,
                stop=not opens,
            )

        nc.vector.tensor_copy(picked_words0[:], words[0][:].indirect(offsets[:]))
        nc.vector.tensor_copy(picked_scales[:], scales[:].indirect(offsets[:]))
        for r in range(4):
            nc.sync.dma_start(
                moved_scales[r:P:QUADRANT, :].bitcast(I32),
                picked_scales[QUADRANT // 2 + r : P : QUADRANT, :].bitcast(I32),
            )
        w2_raw = placed.tile([P, PACK, N], F32, name="w2_raw", align_bytes=256, offset=T)
        nc.sync.dma_start(w2_raw[:], w2.rearrange("(p j) c -> p j c", j=PACK))
        picked_words1 = placed.tile([P, S], U16, name="picked_words1", align_bytes=256, offset=0)
        nc.vector.tensor_copy(picked_words1[:], words[1][:].indirect(offsets[:]))
        cast_w1(nc.scalar.copy, 0, 0, 0, P)
        cast_w1(nc.vector.tensor_copy, 0, 1, 0, M_VECTOR_0)
        cast_w1(nc.scalar.copy, 0, 1, M_VECTOR_0, P)
        for t in range(PACK):
            quantize_w1(0, t)
            first_product(0, t, 0, picked_words0[:, 0:HALF], True)
        for a in range(2):
            cast_w1(nc.vector.tensor_copy, 1, a, 0, M_VECTOR_1[a])
            cast_w1(nc.scalar.copy, 1, a, M_VECTOR_1[a], P)
        for t in range(PACK):
            quantize_w1(1, t)
            first_product(1, t, 0, picked_words1[:, 0:HALF], False)
        for t in range(PACK):
            first_product(1, t, 1, picked_words1[:, HALF:S], True)
            first_product(0, t, 1, picked_words0[:, HALF:S], False)

        w2_bf = keep.tile([P, N, PACK], BF16, name="w2_bf", align_bytes=256)
        w2_codes = keep.tile([P, N], U32, name="w2_codes", align_bytes=256)
        w2_scales = keep.tile([P, N], U8, name="w2_scales", align_bytes=256)
        out_rows = out.rearrange("(b p) j -> p b j", p=P)

        def tap_of(t, d):
            return tap[:, D * t + d : D * t + d + 1]

        def first_tap(half, t):
            j0 = HALF * half + D - 1
            j1 = min(j0 + HALF, S)
            nc.scalar.activation(u[:, t, j0:j1], h[half][t][:, 0 : j1 - j0], COPY, scale=tap_of(t, D - 1))

        def add_tap(half, t, d, j0, j1):
            base = HALF * half + d
            nc.vector.scalar_tensor_tensor(
                out=u[:, t, j0:j1],
                in0=h[half][t][:, j0 - base : j1 - base],
                scalar=vector_tap[:, D * t + d : D * t + d + 1],
                in1=u[:, t, j0:j1],
                op0=MULT,
                op1=ADD,
            )

        def side_product(t, c0):
            nc.scalar.activation(side[:, t, c0:HALF], h[1][t][:, c0:HALF], COPY, scale=tap_of(t, 0))

        def add_side(t0, t1, c0):
            sums = u[:, t0:t1, HALF + c0 : HALF + c0 + CHUNK]
            nc.gpsimd.tensor_tensor(sums, sums, side[:, t0:t1, c0 : c0 + CHUNK], ADD)

        def silu_into(z, j0):
            nc.scalar.activation(
                z.rearrange("p (a i) t -> p a t i", i=4),
                u[:, :, j0 : j0 + z.shape[1]].rearrange("p t (a i) -> p a t i", i=4),
                SILU,
                bias=zero_bias[:],
            )

        def quantized(z, j0):
            codes = keep.tile([P, z.shape[1]], U32, name=f"z_codes{j0}", align_bytes=256)
            plane = keep.tile([P, z.shape[1]], U8, name=f"z_scales{j0}", align_bytes=256)
            nc.vector.quantize_mx(out=codes[:].bitcast(FP8X4), scales=plane[:], in_=z[:].rearrange("p j t -> p (j t)"))
            return codes, plane

        def second_product(acc, b, codes, plane):
            nc.tensor.matmul_mx(
                out=acc,
                lhsT=w2_codes[:, P * b : P * (b + 1)].bitcast(FP8X4),
                lhsT_scale=w2_scales[:, P * b : P * (b + 1)],
                rhs=codes[:].bitcast(FP8X4),
                rhs_scale=plane[:],
                start=True,
                stop=True,
            )

        def both_blocks(z, j0, bank):
            codes, plane = quantized(z, j0)
            acc = psum.tile([P, N // P, z.shape[1]], F32, name=f"acc{j0}", tag=bank)
            for b in range(N // P):
                second_product(acc[:, b, :], b, codes, plane)
            return acc

        def store_both(acc, j0, result, copy):
            copy(result, acc[:])
            nc.sync.dma_start(out_rows[:, :, j0 : j0 + acc.shape[2]], result)

        def cast_w2(copy, c0, c1):
            copy(
                w2_bf[:, c0:c1, :].rearrange("p (a i) j -> p a j i", i=4),
                w2_raw[:, :, c0:c1].rearrange("p j (a i) -> p a j i", i=4),
            )

        for b in range(N // P):
            cast_w2(nc.vector.tensor_copy, P * b, P * (b + 1))
        vector_tap = w2_raw[:, 0, 0 : PACK * D]
        nc.vector.tensor_copy(vector_tap, tap[:])
        for b in range(N // P):
            nc.vector.quantize_mx(
                out=w2_codes[:, P * b : P * (b + 1)].bitcast(FP8X4),
                scales=w2_scales[:, P * b : P * (b + 1)],
                in_=w2_bf[:, P * b : P * (b + 1), :].rearrange("p c j -> p (c j)"),
            )
        side_early = keep.tile([P, 2, HALF], F32, name="side_early", align_bytes=256)
        for t in range(PACK):
            first_tap(0, t)
            if t >= 2:
                nc.scalar.activation(side_early[:, t - 2, :], h[0][t][:], COPY, scale=tap_of(t, 0))
                nc.gpsimd.tensor_tensor(u[:, t, 0:HALF], u[:, t, 0:HALF], side_early[:, t - 2, :], ADD)
        for d in (2, 1):
            for t in (0, 1):
                for c0 in (0, CHUNK):
                    add_tap(0, t, d, c0 + d, c0 + CHUNK + d)
        for t, d in ((0, 0), (2, 2), (1, 0)):
            add_tap(0, t, d, d, HALF + d)
        for c0 in (0, CHUNK):
            add_tap(0, 3, 2, c0 + 2, c0 + CHUNK + 2)
        add_tap(0, 2, 1, 1, HALF + 1)
        side = keep.tile([P, PACK, HALF], F32, name="side", align_bytes=256)
        for t in (0, 1):
            first_tap(1, t)
            side_product(t, 0)
        add_side(0, 2, 0)
        for t in (2, 3):
            first_tap(1, t)
            side_product(t, CHUNK)
        add_side(0, PACK, CHUNK)
        z_early = keep.tile([P, HALF, PACK], BF16, name="z_early", align_bytes=256)
        for j0 in range(0, HALF, CHUNK):
            add_tap(0, 3, 1, max(j0, 1), j0 + CHUNK + j0 // CHUNK)
            silu_into(z_early[:, j0 : j0 + CHUNK, :], j0)
        mid, last, end = HALF, HALF + CHUNK, S - END
        for d in (2, 1):
            for t in (2, 3, 0, 1):
                add_tap(1, t, d, mid + d, last)
        for t in (2, 3):
            add_tap(1, t, 0, mid, last)
        z_mid = keep.tile([P, CHUNK, PACK], BF16, name="z_mid", tag="z_mid", align_bytes=256)
        silu_into(z_mid[:], mid)
        for t in range(PACK):
            add_tap(1, t, 2, last, S)
        codes, plane = quantized(z_early, 0)
        acc_early = [psum.tile([P, HALF], F32, name=f"acc_early{b}", tag=f"bank0_{b}") for b in range(N // P)]
        for b in range(N // P):
            second_product(acc_early[b][:], b, codes, plane)
        z_small = []
        for j0 in (last, end):
            for t in range(PACK):
                add_tap(1, t, 1, j0, j0 + END)
            z_small.append(keep.tile([P, END, PACK], BF16, name=f"z{j0}", tag=f"z{j0}", align_bytes=256))
            silu_into(z_small[-1][:], j0)
        acc_mid = both_blocks(z_mid, mid, "bank0_2")
        early_result = keep.tile([P, HALF], F32, name="early_result", align_bytes=256)
        nc.vector.tensor_copy(early_result[:], acc_early[0][:])
        nc.sync.dma_start(out_rows[:, 0, 0:HALF], early_result[:])
        acc_last = both_blocks(z_small[0], last, "bank0_3")
        second_result = keep.tile([P, HALF], F32, name="second_result", tag="z_mid", align_bytes=256)
        nc.scalar.copy(second_result[:], acc_early[1][:])
        nc.sync.dma_start(out_rows[:, 1, 0:HALF], second_result[:])
        codes, plane = quantized(z_small[1], end)
        acc_end = [psum.tile([P, END], F32, name=f"acc_end{b}", tag=f"bank1_{b}") for b in range(N // P)]
        for b in range(N // P):
            second_product(acc_end[b][:], b, codes, plane)
        store_both(acc_mid, mid, u[:, 1:3, last:S], nc.scalar.copy)
        last_result = keep.tile([P, N // P, CHUNK], F32, name="last_result", tag=f"z{end}", align_bytes=256)
        nc.vector.tensor_copy(last_result[:, :, 0:END], acc_last[:])
        for b in range(N // P):
            nc.vector.tensor_copy(last_result[:, b, END:CHUNK], acc_end[b][:])
            nc.sync.dma_start(out_rows[:, b, last:S], last_result[:, b, :])
